import numpy as np
import ml_dtypes


def mxq(x, axis, fmt="e4m3"):
    dtype, down = {"e4m3": (ml_dtypes.float8_e4m3fn, 7), "e5m2": (ml_dtypes.float8_e5m2, 14)}[fmt]
    v = np.moveaxis(np.asarray(x, np.float32).astype(ml_dtypes.bfloat16).astype(np.float64), axis, -1)
    blocks = v.reshape(v.shape[:-1] + (-1, 32))
    amax = np.abs(blocks).max(-1, keepdims=True)
    byte = np.maximum(np.where(amax > 0, np.frexp(amax)[1] - 1 + 127, 0) - down, 1)
    scale = np.exp2(byte - 127.0)
    codes = (blocks / scale).astype(np.float32).astype(dtype).astype(np.float64)
    return np.moveaxis((codes * scale).reshape(v.shape), -1, axis)


WIDE = False


def mx_kscale(k):
    if not WIDE:
        return np.ones(k)
    levels = np.array([10, -10, 5, -5, 0])
    if k % 512:
        return np.exp2(np.random.permutation(np.resize(levels, k // 32))).repeat(32)
    a = np.empty((k // 512, 16))
    for p in range(k // 512):
        a[p, :8] = np.random.permutation(np.resize(levels, 8))
        for g in range(8):
            far = levels[np.abs(levels - a[p, g]) >= 10]
            a[p, g + 8] = far[np.random.randint(len(far))]
    return np.exp2(a.ravel()).repeat(32)


def f64(x):
    return np.asarray(x).astype(np.float64)


def striped(idx):
    return np.tile(idx.reshape(-1, 16).T, (8, 1)).astype(np.uint16)


def unstriped(offs):
    return offs[:16].T.reshape(-1).astype(np.int64)


E2M1 = np.array([0.0, 0.5, 1.0, 1.5, 2.0, 3.0, 4.0, 6.0, -0.0, -0.5, -1.0, -1.5, -2.0, -3.0, -4.0, -6.0])


def pack_weight(w, fmt):
    k, n = w.shape
    w = f64(np.asarray(w, np.float32).astype(ml_dtypes.bfloat16)).reshape(k // 32, 32, n)
    amax = np.abs(w).max(1)
    if fmt == "e4m3":
        byte = np.frexp(amax)[1] - 1 + 127 - 7
    else:
        mant, ex = np.frexp(amax / 6.0)
        byte = np.where(mant > 0.5, ex, ex - 1) + 127
    byte = np.clip(np.where(amax > 0, byte, 1), 1, 254)
    scaled = (w * np.exp2(127.0 - byte)[:, None, :]).reshape(k, n).astype(np.float32)
    by_word = np.ascontiguousarray(scaled.reshape(k // 512, 128, 4, n).transpose(0, 1, 3, 2))
    if fmt == "e4m3":
        words = by_word.astype(ml_dtypes.float8_e4m3fn).view(np.uint8)
    else:
        c = by_word.astype(ml_dtypes.float4_e2m1fn).view(np.uint8) & 0xF
        words = (c[..., 0::2] | (c[..., 1::2] << 4)).reshape(k // 512, 128, 2 * n)
    return np.ascontiguousarray(words), np.ascontiguousarray(byte.astype(np.uint8).reshape(k // 512, 16, n))


def unpack_weight(words, scales, fmt):
    g, _, n = scales.shape
    words = np.ascontiguousarray(words).reshape(g, 128, n, -1)
    if fmt == "e4m3":
        vals = words.view(ml_dtypes.float8_e4m3fn).astype(np.float64)
    else:
        nib = np.empty((g, 128, n, 4), np.uint8)
        nib[..., 0::2] = words & 0xF
        nib[..., 1::2] = words >> 4
        vals = E2M1[nib]
    vals = vals * np.repeat(np.exp2(scales.astype(np.float64) - 127.0), 8, axis=1)[..., None]
    return vals.transpose(0, 1, 3, 2).reshape(g * 512, n)


K, T, E, C, H, N = 512, 1024, 2, 256, 512, 512


def by_expert(wq, xq):
    return np.concatenate([wq[e].T @ xq[:, e * C:(e + 1) * C] for e in range(E)], axis=1)


def setup_inputs():
    n = np.random.standard_normal
    v = mx_kscale(N)
    u = mx_kscale(H)
    slot_token = np.random.permutation(T)[:E * C]
    w_slot = np.random.uniform(0.2, 1.0, E * C)
    partner = np.random.permutation(T)[:E * C]
    dy = pack_weight(n((N, T)) * v[:, None], "e4m3")
    w2t = [pack_weight(m, "e2m1") for m in n((E, N, H)) / np.sqrt(N) / v[None, :, None] * u]
    w1t = [pack_weight(m, "e2m1") for m in n((E, H, K)) / np.sqrt(H) / u[None, :, None]]
    wpt = [pack_weight(m, "e2m1") for m in n((E, H, K)) / np.sqrt(H) / u[None, :, None]]
    return {
        "dy_words": dy[0],
        "dy_scales": dy[1],
        "w2t_words": np.stack([m[0] for m in w2t]),
        "w2t_scales": np.stack([m[1] for m in w2t]),
        "w1t_words": np.stack([m[0] for m in w1t]),
        "w1t_scales": np.stack([m[1] for m in w1t]),
        "wpt_words": np.stack([m[0] for m in wpt]),
        "wpt_scales": np.stack([m[1] for m in wpt]),
        "gate": (np.tile(w_slot, (128, 1))).astype(np.float32),
        "offs": striped(slot_token),
        "offs2": striped(partner),
    }


def reference(dy_words, dy_scales, w2t_words, w2t_scales, w1t_words, w1t_scales, wpt_words, wpt_scales, gate, offs, offs2):
    w2t = np.stack([unpack_weight(w2t_words[e], w2t_scales[e], "e2m1") for e in range(E)])
    w1t = np.stack([unpack_weight(w1t_words[e], w1t_scales[e], "e2m1") for e in range(E)])
    wpt = np.stack([unpack_weight(wpt_words[e], wpt_scales[e], "e2m1") for e in range(E)])
    idx, idx2 = unstriped(offs), unstriped(offs2)
    gq = unpack_weight(dy_words, dy_scales, "e4m3")[:, idx]
    dh = f64(gate[:1]) * by_expert(w2t, gq)
    dq = mxq(dh, 0, "e4m3")
    out = np.zeros((K, T))
    out[:, idx] = by_expert(w1t, dq)
    out[:, idx2] += by_expert(wpt, dq)
    return out

@@ -1,0 +1,204 @@
+from contextlib import ExitStack
+
+import concourse.mybir as mybir
+from concourse.masks import make_identity
+
+K, T, E, C, H, N = 512, 1024, 2, 256, 512, 512
+S = E * C
+FLOPS = 2 * S * (N * H + 2 * H * K)
+
+F32 = mybir.dt.float32
+BF16 = mybir.dt.bfloat16
+I32 = mybir.dt.int32
+U32 = mybir.dt.uint32
+U16 = mybir.dt.uint16
+U8 = mybir.dt.uint8
+FP8X4 = mybir.dt.float8_e4m3fn_x4
+FP4X4 = mybir.dt.float4_e2m1fn_x4
+COPY = mybir.ActivationFunctionType.Copy
+ADD = mybir.AluOpType.add
+
+P = 128
+CH = 128
+BANK = 512
+
+
+def tile_moe_dub_none_kernel(
+    tc, dy_words, dy_scales, w2t_words, w2t_scales, w1t_words, w1t_scales, wpt_words, wpt_scales, gate, offs, offs2, out
+):
+    nc = tc.nc
+    with ExitStack() as ctx:
+        keep = ctx.enter_context(tc.tile_pool(name="keep", bufs=1))
+        ring = ctx.enter_context(tc.tile_pool(name="ring", bufs=2))
+        psa = ctx.enter_context(tc.psum_pool(name="psa", bufs=2))
+        psy = ctx.enter_context(tc.psum_pool(name="psy", bufs=2))
+        psk = ctx.enter_context(tc.psum_pool(name="psk", bufs=1))
+
+        tok = keep.tile([P, S // 16], U16, name="tok")
+        par = keep.tile([P, S // 16], U16, name="par")
+        dyw = keep.tile([P, T], I32, name="dyw", align_bytes=64)
+        dys = keep.tile([P, T], U8, name="dys", align_bytes=64)
+        gw = keep.tile([P, S], U32, name="gw", align_bytes=64)
+        gs = keep.tile([P, S], U8, name="gs", align_bytes=64)
+        w2w = keep.tile([P, E, 2 * H], U8, name="w2w", align_bytes=64)
+        w1w = keep.tile([P, E, 2 * K], U8, name="w1w", align_bytes=64)
+        wpw = keep.tile([P, E, 2 * K], U8, name="wpw", align_bytes=64)
+        w2s = keep.tile([P, E, H], U8, name="w2s", align_bytes=64)
+        w1s = keep.tile([P, E, K], U8, name="w1s", align_bytes=64)
+        wps = keep.tile([P, E, K], U8, name="wps", align_bytes=64)
+        grows = keep.tile([P, P], F32, name="grows")
+        gcol = keep.tile([P, S // CH], F32, name="gcol")
+        ident = keep.tile([P, P], F32, name="ident")
+        dqw = keep.tile([P, S], U32, name="dqw", align_bytes=64)
+        dqs = keep.tile([P, S], U8, name="dqs", align_bytes=64)
+        winx = [keep.tile([P, T], F32, name="winx%d" % b) for b in range(2)]
+        winp = [keep.tile([P, T], F32, name="winp%d" % b) for b in range(2)]
+
+        adder = [psk.tile([P, BANK], F32, name="adder%d" % h) for h in range(T // BANK)]
+
+        def load_words(tile, words):
+            nc.sync.dma_start(tile[:].bitcast(I32), words[:, 0].rearrange("e p n -> p e n").bitcast(I32))
+
+        def load_scales(tile, scales, queues):
+            for q, queue in enumerate(queues):
+                queue.dma_start(
+                    tile[32 * q : 32 * q + 4].bitcast(I32),
+                    scales[:, 0, 4 * q : 4 * q + 4, :].rearrange("e r n -> r e n").bitcast(I32),
+                )
+
+        nc.vector.memset(dys[:].bitcast(I32), 0)
+        for plane in (w2s, w1s, wps):
+            nc.vector.memset(plane[:].rearrange("p e n -> p (e n)").bitcast(I32), 0)
+        nc.sync.dma_start(tok[:], offs)
+        nc.sync.dma_start(grows[:], gate.rearrange("r (c j) -> (r c) j", j=CH)[0:P, :])
+        nc.sync.dma_start(dyw[:], dy_words[0].rearrange("p t d -> p (t d)").bitcast(I32))
+        load_words(w2w, w2t_words)
+        for q in range(4):
+            nc.scalar.dma_start(dys[32 * q : 32 * q + 4].bitcast(I32), dy_scales[0, 4 * q : 4 * q + 4, :].bitcast(I32))
+        load_scales(w2s, w2t_scales, (nc.sync, nc.sync, nc.gpsimd, nc.gpsimd))
+        make_identity(nc, ident[:])
+        load_words(w1w, w1t_words)
+        load_words(wpw, wpt_words)
+        load_scales(w1s, w1t_scales, (nc.sync,) * 4)
+        nc.sync.dma_start(par[:], offs2)
+        load_scales(wps, wpt_scales, (nc.sync, nc.sync, nc.gpsimd, nc.gpsimd))
+
+        nc.vector.memset(winx[0][:], 0.0)
+        nc.vector.memset(winp[0][:], 0.0)
+        nc.scalar.activation(winx[1][:], winx[0][:], COPY)
+
+        gt = psa.tile([P, P], F32, name="gt", tag="tr")
+        nc.tensor.transpose(gt[:], grows[:], ident[:])
+        nc.scalar.copy(gcol[:], gt[:, 0 : S // CH])
+
+        def gather(a, b):
+            lst = tok[:, a // 16 : b // 16]
+            nc.vector.tensor_copy(gs[:, a:b], dys[:].indirect(lst))
+            nc.vector.tensor_copy(gw[:, a:b], dyw[:].bitcast(U32).indirect(lst))
+
+        def hidden(c, mover):
+            e = c * CH // C
+            cols = slice(c * CH, (c + 1) * CH)
+            acc = psa.tile([P, H], F32, name="acc", tag="acc")
+            nc.tensor.matmul_mx(
+                out=acc[:], lhsT=gw[:, cols].bitcast(FP8X4), lhsT_scale=gs[:, cols],
+                rhs=w2w[:, e, :].bitcast(FP4X4), rhs_scale=w2s[:, e, :], start=True, stop=True,
+            )
+            dh = ring.tile([P, H], BF16, name="dh", tag="dh")
+            nc.scalar.activation(
+                dh[:].rearrange("s (u p d) -> s u p d", u=2, d=2),
+                acc[:].rearrange("s (p u d) -> s u p d", u=2, d=2),
+                COPY, scale=gcol[:, c : c + 1],
+            )
+            pairs = dh[:].bitcast(F32)
+            turned = psa.tile([P, 2, CH], F32, name="turned", tag="tr")
+            for u in range(2):
+                nc.tensor.transpose(turned[:, u, :], pairs[:, u * P : (u + 1) * P], ident[:])
+            quads = keep.tile([P, 4 * CH], BF16, name="quads%d" % c, align_bytes=64)
+            mover(quads[:].bitcast(F32).rearrange("p (s u) -> p s u", u=2), turned[:].rearrange("p u s -> p s u"))
+            return quads
+
+        def quantise(c, quads):
+            cols = slice(c * CH, (c + 1) * CH)
+            nc.vector.quantize_mx(out=dqw[:, cols].bitcast(FP8X4), scales=dqs[:, cols], in_=quads[:])
+
+        def product(dst, ww, ws, m, a, b):
+            e = a // C
+            nc.tensor.matmul_mx(
+                out=dst, lhsT=ww[:, e, 2 * P * m : 2 * P * (m + 1)].bitcast(FP4X4), lhsT_scale=ws[:, e, P * m : P * (m + 1)],
+                rhs=dqw[:, a:b].bitcast(FP8X4), rhs_scale=dqs[:, a:b], start=True, stop=True,
+            )
+
+        def both(m, a, b):
+            n = b - a
+            y = psy.tile([P, 2, n], F32, name="y", tag="y")
+            product(y[:, 0, :], w1w, w1s, m, a, b)
+            product(y[:, 1, :], wpw, wps, m, a, b)
+            ys = keep.tile([P, 2, n], F32, name="ys%d_%d" % (m, a))
+            nc.scalar.copy(ys[:], y[:])
+            return ys
+
+        def whole(ww, ws, m, label):
+            y = psy.tile([P, S], F32, name="y", tag="y")
+            for e in range(E):
+                product(y[:, e * C : (e + 1) * C], ww, ws, m, e * C, (e + 1) * C)
+            ys = keep.tile([P, S], F32, name="%s%d" % (label, m))
+            nc.scalar.copy(ys[:], y[:])
+            return ys
+
+        def scatter(win, lst, a, b, src):
+            nc.vector.tensor_copy(win[:].indirect(lst[:, a // 16 : b // 16]), src)
+
+        def scatter_both(a, b, ys):
+            scatter(winx[0], tok, a, b, ys[:, 0, :])
+            scatter(winp[0], par, a, b, ys[:, 1, :])
+
+        def add_on_tensor(m):
+            wx, wp = winx[m % 2], winp[m % 2]
+            flipped = []
+            for h in range(T // BANK):
+                for j in range(BANK // P):
+                    blk = slice(h * BANK + j * P, h * BANK + (j + 1) * P)
+                    dst = adder[h][:, j * P : (j + 1) * P]
+                    nc.tensor.matmul(dst, lhsT=wx[:, blk], rhs=ident[:], start=True, stop=False, is_transpose=True)
+                    nc.tensor.matmul(dst, lhsT=wp[:, blk], rhs=ident[:], start=False, stop=True, is_transpose=True)
+                flipped.append(ring.tile([P, BANK], F32, name="flipped", tag="flipped"))
+                nc.scalar.copy(flipped[h][:], adder[h][:])
+            for h in range(T // BANK):
+                for j in range(BANK // P):
+                    nc.tensor.transpose(adder[h][:, j * P : (j + 1) * P], flipped[h][:, j * P : (j + 1) * P], ident[:])
+                res = ring.tile([P, BANK], F32, name="res", tag="res")
+                nc.scalar.copy(res[:], adder[h][:])
+                nc.scalar.dma_start(out[m * P : (m + 1) * P, h * BANK : (h + 1) * BANK], res[:])
+
+        gather(0, CH)
+        q0 = hidden(0, nc.vector.tensor_copy)
+        gather(CH, C)
+        q1 = hidden(1, nc.vector.tensor_copy)
+        gather(C, S)
+        nc.vector.memset(winp[1][:], 0.0)
+        quantise(0, q0)
+        y0 = both(0, 0, CH)
+        q2 = hidden(2, nc.scalar.copy)
+        quantise(1, q1)
+        y1 = both(0, CH, C)
+        q3 = hidden(3, nc.scalar.copy)
+        scatter_both(0, CH, y0)
+        quantise(2, q2)
+        scatter_both(CH, C, y1)
+        quantise(3, q3)
+        y2 = both(0, C, S)
+        later = {}
+        for m in range(1, K // P):
+            later[m] = (whole(w1w, w1s, m, "yx"), whole(wpw, wps, m, "yp"))
+        scatter_both(C, S, y2)
+        for m in range(1, K // P):
+            scatter(winx[m % 2], tok, 0, S, later[m][0][:])
+            add_on_tensor(m - 1)
+            scatter(winp[m % 2], par, 0, S, later[m][1][:])
+        m = K // P - 1
+        last = keep.tile([P, T], F32, name="last")
+        for h in range(4):
+            cols = slice(h * 256, (h + 1) * 256)
+            nc.vector.tensor_tensor(last[:, cols], winx[m % 2][:, cols], winp[m % 2][:, cols], ADD)
+            nc.sync.dma_start(out[m * P : (m + 1) * P, cols], last[:, cols])

@@ -17,6 +17,7 @@ FP8X4 = mybir.dt.float8_e4m3fn_x4
 FP4X4 = mybir.dt.float4_e2m1fn_x4
 COPY = mybir.ActivationFunctionType.Copy
 ADD = mybir.AluOpType.add
+MULT = mybir.AluOpType.mult
 
 P = 128
 CH = 128
@@ -30,19 +31,17 @@ def tile_moe_dub_none_kernel(
     with ExitStack() as ctx:
         keep = ctx.enter_context(tc.tile_pool(name="keep", bufs=1))
         ring = ctx.enter_context(tc.tile_pool(name="ring", bufs=2))
-        psa = ctx.enter_context(tc.psum_pool(name="psa", bufs=2))
+        early = ctx.enter_context(tc.tile_pool(name="early", bufs=1))
+        psa = ctx.enter_context(tc.psum_pool(name="psa", bufs=4))
+        pst = ctx.enter_context(tc.psum_pool(name="pst", bufs=2))
         psy = ctx.enter_context(tc.psum_pool(name="psy", bufs=2))
-        psk = ctx.enter_context(tc.psum_pool(name="psk", bufs=1))
 
         tok = keep.tile([P, S // 16], U16, name="tok")
         par = keep.tile([P, S // 16], U16, name="par")
-        dyw = keep.tile([P, T], I32, name="dyw", align_bytes=64)
+        blank = early.tile([P, P], F32, name="blank", align_bytes=64, offset=4 * T - 2 * P)
         dys = keep.tile([P, T], U8, name="dys", align_bytes=64)
-        gw = keep.tile([P, S], U32, name="gw", align_bytes=64)
-        gs = keep.tile([P, S], U8, name="gs", align_bytes=64)
-        w2w = keep.tile([P, E, 2 * H], U8, name="w2w", align_bytes=64)
-        w1w = keep.tile([P, E, 2 * K], U8, name="w1w", align_bytes=64)
-        wpw = keep.tile([P, E, 2 * K], U8, name="wpw", align_bytes=64)
+        gw = [keep.tile([P, C], U32, name="gw%d" % e, align_bytes=64) for e in range(E)]
+        gs = [keep.tile([P, C], U8, name="gs%d" % e, align_bytes=64) for e in range(E)]
         w2s = keep.tile([P, E, H], U8, name="w2s", align_bytes=64)
         w1s = keep.tile([P, E, K], U8, name="w1s", align_bytes=64)
         wps = keep.tile([P, E, K], U8, name="wps", align_bytes=64)
@@ -54,68 +53,86 @@ def tile_moe_dub_none_kernel(
         winx = [keep.tile([P, T], F32, name="winx%d" % b) for b in range(2)]
         winp = [keep.tile([P, T], F32, name="winp%d" % b) for b in range(2)]
 
-        adder = [psk.tile([P, BANK], F32, name="adder%d" % h) for h in range(T // BANK)]
 
         def load_words(tile, words):
-            nc.sync.dma_start(tile[:].bitcast(I32), words[:, 0].rearrange("e p n -> p e n").bitcast(I32))
+            nc.sync.dma_start(tile.bitcast(I32), words[:, 0].rearrange("e p n -> p e n").bitcast(I32))
 
-        def load_scales(tile, scales, queues):
-            for q, queue in enumerate(queues):
-                queue.dma_start(
+        def load_scales(tile, scales):
+            for q in range(4):
+                nc.sync.dma_start(
                     tile[32 * q : 32 * q + 4].bitcast(I32),
                     scales[:, 0, 4 * q : 4 * q + 4, :].rearrange("e r n -> r e n").bitcast(I32),
                 )
 
-        nc.vector.memset(dys[:].bitcast(I32), 0)
-        for plane in (w2s, w1s, wps):
+        def zero_plane(plane):
             nc.vector.memset(plane[:].rearrange("p e n -> p (e n)").bitcast(I32), 0)
+
+        nc.vector.memset(blank[:], 0.0)
+        nc.vector.memset(dys[:].bitcast(I32), 0)
+        nc.vector.tensor_copy(ident[:], blank[:])
+        zero_plane(w2s)
+        zero_plane(w1s)
+        zero_plane(wps)
+        make_identity(nc, ident[:], nomemset=True)
+        dyw = early.tile([P, T], I32, name="dyw", align_bytes=64, offset=0)
+        wall = early.tile([P, 3, E, 2 * H], U8, name="wall", align_bytes=64, offset=4 * T)
+        w2w, w1w, wpw = wall[:, 0], wall[:, 1], wall[:, 2]
         nc.sync.dma_start(tok[:], offs)
         nc.sync.dma_start(grows[:], gate.rearrange("r (c j) -> (r c) j", j=CH)[0:P, :])
-        nc.sync.dma_start(dyw[:], dy_words[0].rearrange("p t d -> p (t d)").bitcast(I32))
-        load_words(w2w, w2t_words)
-        for q in range(4):
-            nc.scalar.dma_start(dys[32 * q : 32 * q + 4].bitcast(I32), dy_scales[0, 4 * q : 4 * q + 4, :].bitcast(I32))
-        load_scales(w2s, w2t_scales, (nc.sync, nc.sync, nc.gpsimd, nc.gpsimd))
-        make_identity(nc, ident[:])
-        load_words(w1w, w1t_words)
-        load_words(wpw, wpt_words)
-        load_scales(w1s, w1t_scales, (nc.sync,) * 4)
         nc.sync.dma_start(par[:], offs2)
-        load_scales(wps, wpt_scales, (nc.sync, nc.sync, nc.gpsimd, nc.gpsimd))
-
+        for q in range(4):
+            nc.sync.dma_start(dys[32 * q : 32 * q + 4].bitcast(I32), dy_scales[0, 4 * q : 4 * q + 4, :].bitcast(I32))
+        nc.sync.dma_start(dyw[:], dy_words[0].rearrange("p t d -> p (t d)").bitcast(I32))
+        nc.sync.dma_start(w2w[:, 0].bitcast(I32), w2t_words[0, 0].bitcast(I32))
+        load_scales(w2s, w2t_scales)
+        nc.sync.dma_start(w2w[:, 1].bitcast(I32), w2t_words[1, 0].bitcast(I32))
+        load_words(w1w, w1t_words)
+        load_scales(w1s, w1t_scales)
+        load_words(wpw, wpt_words)
+        load_scales(wps, wpt_scales)
         nc.vector.memset(winx[0][:], 0.0)
         nc.vector.memset(winp[0][:], 0.0)
         nc.scalar.activation(winx[1][:], winx[0][:], COPY)
+        nc.gpsimd.memset(winp[1][:], 0.0)
 
-        gt = psa.tile([P, P], F32, name="gt", tag="tr")
+        gt = pst.tile([P, P], F32, name="gt", tag="tr")
         nc.tensor.transpose(gt[:], grows[:], ident[:])
         nc.scalar.copy(gcol[:], gt[:, 0 : S // CH])
 
-        def gather(a, b):
-            lst = tok[:, a // 16 : b // 16]
-            nc.vector.tensor_copy(gs[:, a:b], dys[:].indirect(lst))
-            nc.vector.tensor_copy(gw[:, a:b], dyw[:].bitcast(U32).indirect(lst))
+        def gather_words(a, b):
+            e = a // C
+            nc.vector.tensor_copy(gw[e][:, a - e * C : b - e * C], dyw[:].bitcast(U32).indirect(tok[:, a // 16 : b // 16]))
 
-        def hidden(c, mover):
+        def spare():
+            return psa.tile([P, BANK], F32, name="acc", tag="acc")
+
+        def gather_scales(e):
+            nc.vector.tensor_copy(gs[e][:], dys[:].indirect(tok[:, e * C // 16 : (e + 1) * C // 16]))
+
+        def hidden(c):
             e = c * CH // C
-            cols = slice(c * CH, (c + 1) * CH)
-            acc = psa.tile([P, H], F32, name="acc", tag="acc")
+            own = slice(c * CH - e * C, (c + 1) * CH - e * C)
+            acc = spare()
             nc.tensor.matmul_mx(
-                out=acc[:], lhsT=gw[:, cols].bitcast(FP8X4), lhsT_scale=gs[:, cols],
+                out=acc[:], lhsT=gw[e][:, own].bitcast(FP8X4), lhsT_scale=gs[e][:, own],
                 rhs=w2w[:, e, :].bitcast(FP4X4), rhs_scale=w2s[:, e, :], start=True, stop=True,
             )
-            dh = ring.tile([P, H], BF16, name="dh", tag="dh")
-            nc.scalar.activation(
-                dh[:].rearrange("s (u p d) -> s u p d", u=2, d=2),
-                acc[:].rearrange("s (p u d) -> s u p d", u=2, d=2),
-                COPY, scale=gcol[:, c : c + 1],
-            )
+            dh = keep.tile([P, H], BF16, name="dh%d" % c)
+            dst = dh[:].rearrange("s (u p d) -> s u p d", u=2, d=2)
+            src = acc[:].rearrange("s (p u d) -> s u p d", u=2, d=2)
+            if c < 3:
+                nc.scalar.activation(dst, src, COPY, scale=gcol[:, c : c + 1])
+            else:
+                nc.vector.tensor_scalar(dst, src, gcol[:, c : c + 1], None, MULT)
+            return dh
+
+        def turn(c, dh):
             pairs = dh[:].bitcast(F32)
-            turned = psa.tile([P, 2, CH], F32, name="turned", tag="tr")
+            turned = pst.tile([P, 2, CH], F32, name="turned", tag="tr")
             for u in range(2):
                 nc.tensor.transpose(turned[:, u, :], pairs[:, u * P : (u + 1) * P], ident[:])
             quads = keep.tile([P, 4 * CH], BF16, name="quads%d" % c, align_bytes=64)
-            mover(quads[:].bitcast(F32).rearrange("p (s u) -> p s u", u=2), turned[:].rearrange("p u s -> p s u"))
+            nc.vector.tensor_copy(quads[:].bitcast(F32).rearrange("p (s u) -> p s u", u=2), turned[:].rearrange("p u s -> p s u"))
             return quads
 
         def quantise(c, quads):
@@ -129,31 +146,32 @@ def tile_moe_dub_none_kernel(
                 rhs=dqw[:, a:b].bitcast(FP8X4), rhs_scale=dqs[:, a:b], start=True, stop=True,
             )
 
-        def both(m, a, b):
-            n = b - a
-            y = psy.tile([P, 2, n], F32, name="y", tag="y")
-            product(y[:, 0, :], w1w, w1s, m, a, b)
-            product(y[:, 1, :], wpw, wps, m, a, b)
-            ys = keep.tile([P, 2, n], F32, name="ys%d_%d" % (m, a))
-            nc.scalar.copy(ys[:], y[:])
-            return ys
+        def fresh():
+            return psy.tile([P, BANK], F32, name="y", tag="y")
 
-        def whole(ww, ws, m, label):
-            y = psy.tile([P, S], F32, name="y", tag="y")
-            for e in range(E):
-                product(y[:, e * C : (e + 1) * C], ww, ws, m, e * C, (e + 1) * C)
-            ys = keep.tile([P, S], F32, name="%s%d" % (label, m))
-            nc.scalar.copy(ys[:], y[:])
-            return ys
+        def results(y, jobs):
+            at = 0
+            for side, m, a, b in jobs:
+                for lo in range(a, b, C):
+                    hi = min(b, lo + C)
+                    product(y[:, at : at + hi - lo], sides[side][0], sides[side][1], m, lo, hi)
+                    at += hi - lo
+            ys = keep.tile([P, at], F32, name="ys", tag="ys%d_%d_%d" % jobs[0][:3])
+            nc.scalar.copy(ys[:], y[:, 0:at])
+            at = 0
+            pieces = []
+            for side, m, a, b in jobs:
+                pieces.append((side, m, a, b, ys[:, at : at + b - a]))
+                at += b - a
+            return pieces
 
-        def scatter(win, lst, a, b, src):
-            nc.vector.tensor_copy(win[:].indirect(lst[:, a // 16 : b // 16]), src)
+        sides = ((w1w, w1s, tok, winx), (wpw, wps, par, winp))
 
-        def scatter_both(a, b, ys):
-            scatter(winx[0], tok, a, b, ys[:, 0, :])
-            scatter(winp[0], par, a, b, ys[:, 1, :])
+        def scatter(piece):
+            side, m, a, b, src = piece
+            nc.vector.tensor_copy(sides[side][3][m % len(sides[side][3])][:].indirect(sides[side][2][:, a // 16 : b // 16]), src)
 
-        def add_on_tensor(m):
+        def add_on_tensor(m, adder):
             wx, wp = winx[m % 2], winp[m % 2]
             flipped = []
             for h in range(T // BANK):
@@ -171,31 +189,25 @@ def tile_moe_dub_none_kernel(
                 nc.scalar.copy(res[:], adder[h][:])
                 nc.scalar.dma_start(out[m * P : (m + 1) * P, h * BANK : (h + 1) * BANK], res[:])
 
-        gather(0, CH)
-        q0 = hidden(0, nc.vector.tensor_copy)
-        gather(CH, C)
-        q1 = hidden(1, nc.vector.tensor_copy)
-        gather(C, S)
-        nc.vector.memset(winp[1][:], 0.0)
-        quantise(0, q0)
-        y0 = both(0, 0, CH)
-        q2 = hidden(2, nc.scalar.copy)
-        quantise(1, q1)
-        y1 = both(0, CH, C)
-        q3 = hidden(3, nc.scalar.copy)
-        scatter_both(0, CH, y0)
-        quantise(2, q2)
-        scatter_both(CH, C, y1)
-        quantise(3, q3)
-        y2 = both(0, C, S)
-        later = {}
+        gather_scales(0)
+        gather_words(0, CH)
+        gather_words(CH, C)
+        gather_scales(1)
+        gather_words(C, S)
+        dhs = [hidden(c) for c in range(S // CH)]
+        for c in range(S // CH):
+            quantise(c, turn(c, dhs[c]))
+        todo = results(fresh(), [(0, 0, 0, C)]) + results(fresh(), [(1, 0, 0, C)])
+        adder = [spare() for h in range(T // BANK)]
+        todo += results(spare(), [(0, 0, C, S), (1, 0, C, S)])
         for m in range(1, K // P):
-            later[m] = (whole(w1w, w1s, m, "yx"), whole(wpw, wps, m, "yp"))
-        scatter_both(C, S, y2)
+            todo += results(fresh(), [(0, m, 0, S)]) + results(spare(), [(1, m, 0, S)])
+        for piece in todo[:4]:
+            scatter(piece)
         for m in range(1, K // P):
-            scatter(winx[m % 2], tok, 0, S, later[m][0][:])
-            add_on_tensor(m - 1)
-            scatter(winp[m % 2], par, 0, S, later[m][1][:])
+            scatter(todo[2 * m + 2])
+            add_on_tensor(m - 1, adder)
+            scatter(todo[2 * m + 3])
         m = K // P - 1
         last = keep.tile([P, T], F32, name="last")
         for h in range(4):

@@ -78,26 +78,26 @@ def tile_moe_dub_none_kernel(
         wall = early.tile([P, 3, E, 2 * H], U8, name="wall", align_bytes=64, offset=4 * T)
         w2w, w1w, wpw = wall[:, 0], wall[:, 1], wall[:, 2]
         nc.sync.dma_start(tok[:], offs)
-        nc.sync.dma_start(grows[:], gate.rearrange("r (c j) -> (r c) j", j=CH)[0:P, :])
-        nc.sync.dma_start(par[:], offs2)
         for q in range(4):
             nc.sync.dma_start(dys[32 * q : 32 * q + 4].bitcast(I32), dy_scales[0, 4 * q : 4 * q + 4, :].bitcast(I32))
+        nc.sync.dma_start(grows[:], gate.rearrange("r (c j) -> (r c) j", j=CH)[0:P, :])
         nc.sync.dma_start(dyw[:], dy_words[0].rearrange("p t d -> p (t d)").bitcast(I32))
         nc.sync.dma_start(w2w[:, 0].bitcast(I32), w2t_words[0, 0].bitcast(I32))
         load_scales(w2s, w2t_scales)
+        nc.sync.dma_start(par[:], offs2)
         nc.sync.dma_start(w2w[:, 1].bitcast(I32), w2t_words[1, 0].bitcast(I32))
         load_words(w1w, w1t_words)
         load_scales(w1s, w1t_scales)
         load_words(wpw, wpt_words)
         load_scales(wps, wpt_scales)
         nc.vector.memset(winx[0][:], 0.0)
-        nc.vector.memset(winp[0][:], 0.0)
-        nc.scalar.activation(winx[1][:], winx[0][:], COPY)
+        nc.scalar.activation(winp[0][:], winx[0][:], COPY)
         nc.gpsimd.memset(winp[1][:], 0.0)
 
         gt = pst.tile([P, P], F32, name="gt", tag="tr")
         nc.tensor.transpose(gt[:], grows[:], ident[:])
         nc.scalar.copy(gcol[:], gt[:, 0 : S // CH])
+        nc.scalar.copy(winx[1][:], winx[0][:])
 
         def gather_words(a, b):
             e = a // C
@@ -120,7 +120,7 @@ def tile_moe_dub_none_kernel(
             dh = keep.tile([P, H], BF16, name="dh%d" % c)
             dst = dh[:].rearrange("s (u p d) -> s u p d", u=2, d=2)
             src = acc[:].rearrange("s (p u d) -> s u p d", u=2, d=2)
-            if c < 3:
+            if c % 2 == 0:
                 nc.scalar.activation(dst, src, COPY, scale=gcol[:, c : c + 1])
             else:
                 nc.vector.tensor_scalar(dst, src, gcol[:, c : c + 1], None, MULT)
@@ -132,7 +132,7 @@ def tile_moe_dub_none_kernel(
             for u in range(2):
                 nc.tensor.transpose(turned[:, u, :], pairs[:, u * P : (u + 1) * P], ident[:])
             quads = keep.tile([P, 4 * CH], BF16, name="quads%d" % c, align_bytes=64)
-            nc.vector.tensor_copy(quads[:].bitcast(F32).rearrange("p (s u) -> p s u", u=2), turned[:].rearrange("p u s -> p s u"))
+            nc.scalar.copy(quads[:].bitcast(F32).rearrange("p (s u) -> p s u", u=2), turned[:].rearrange("p u s -> p s u"))
             return quads
 
         def quantise(c, quads):

@@ -31,21 +31,19 @@ def tile_moe_dub_none_kernel(
     with ExitStack() as ctx:
         keep = ctx.enter_context(tc.tile_pool(name="keep", bufs=1))
         ring = ctx.enter_context(tc.tile_pool(name="ring", bufs=2))
-        early = ctx.enter_context(tc.tile_pool(name="early", bufs=1))
-        psa = ctx.enter_context(tc.psum_pool(name="psa", bufs=4))
-        pst = ctx.enter_context(tc.psum_pool(name="pst", bufs=2))
-        psy = ctx.enter_context(tc.psum_pool(name="psy", bufs=2))
+        words = ctx.enter_context(tc.tile_pool(name="words", bufs=1))
+        ps = ctx.enter_context(tc.psum_pool(name="ps", bufs=1))
 
         tok = keep.tile([P, S // 16], U16, name="tok")
         par = keep.tile([P, S // 16], U16, name="par")
-        blank = early.tile([P, P], F32, name="blank", align_bytes=64, offset=4 * T - 2 * P)
+        dyw = keep.tile([P, T], I32, name="dyw", align_bytes=64)
         dys = keep.tile([P, T], U8, name="dys", align_bytes=64)
-        gw = [keep.tile([P, C], U32, name="gw%d" % e, align_bytes=64) for e in range(E)]
-        gs = [keep.tile([P, C], U8, name="gs%d" % e, align_bytes=64) for e in range(E)]
+        w2w = keep.tile([P, E, 2 * H], U8, name="w2w", align_bytes=64)
+        w1w = keep.tile([P, E, 2 * K], U8, name="w1w", align_bytes=64)
+        wpw = keep.tile([P, E, 2 * K], U8, name="wpw", align_bytes=64)
         w2s = keep.tile([P, E, H], U8, name="w2s", align_bytes=64)
         w1s = keep.tile([P, E, K], U8, name="w1s", align_bytes=64)
         wps = keep.tile([P, E, K], U8, name="wps", align_bytes=64)
-        grows = keep.tile([P, P], F32, name="grows")
         gcol = keep.tile([P, S // CH], F32, name="gcol")
         ident = keep.tile([P, P], F32, name="ident")
         dqw = keep.tile([P, S], U32, name="dqw", align_bytes=64)
@@ -53,164 +51,174 @@ def tile_moe_dub_none_kernel(
         winx = [keep.tile([P, T], F32, name="winx%d" % b) for b in range(2)]
         winp = [keep.tile([P, T], F32, name="winp%d" % b) for b in range(2)]
 
+        banks = [ps.tile([P, BANK], F32, name="bank%d" % b) for b in range(8)]
 
         def load_words(tile, words):
-            nc.sync.dma_start(tile.bitcast(I32), words[:, 0].rearrange("e p n -> p e n").bitcast(I32))
+            nc.sync.dma_start(tile[:].bitcast(I32), words[:, 0].rearrange("e p n -> p e n").bitcast(I32))
+
+        def load_rows(queue, tile, scales, q):
+            queue.dma_start(
+                tile[32 * q : 32 * q + 4].bitcast(I32),
+                scales[:, 0, 4 * q : 4 * q + 4, :].rearrange("e r n -> r e n").bitcast(I32),
+            )
 
         def load_scales(tile, scales):
             for q in range(4):
-                nc.sync.dma_start(
-                    tile[32 * q : 32 * q + 4].bitcast(I32),
-                    scales[:, 0, 4 * q : 4 * q + 4, :].rearrange("e r n -> r e n").bitcast(I32),
-                )
+                load_rows(nc.sync, tile, scales, q)
 
-        def zero_plane(plane):
-            nc.vector.memset(plane[:].rearrange("p e n -> p (e n)").bitcast(I32), 0)
+        def load_dy_rows(queue, q):
+            queue.dma_start(dys[32 * q : 32 * q + 4].bitcast(I32), dy_scales[0, 4 * q : 4 * q + 4, :].bitcast(I32))
 
-        nc.vector.memset(blank[:], 0.0)
         nc.vector.memset(dys[:].bitcast(I32), 0)
-        nc.vector.tensor_copy(ident[:], blank[:])
-        zero_plane(w2s)
-        zero_plane(w1s)
-        zero_plane(wps)
+        nc.vector.memset(ident[:], 0.0)
         make_identity(nc, ident[:], nomemset=True)
-        dyw = early.tile([P, T], I32, name="dyw", align_bytes=64, offset=0)
-        wall = early.tile([P, 3, E, 2 * H], U8, name="wall", align_bytes=64, offset=4 * T)
-        w2w, w1w, wpw = wall[:, 0], wall[:, 1], wall[:, 2]
+        nc.vector.memset(winx[0][:], 0.0)
+        nc.gpsimd.memset(winp[1][:], 0.0)
+        load_rows(nc.scalar, w2s, w2t_scales, 0)
         nc.sync.dma_start(tok[:], offs)
-        for q in range(4):
-            nc.sync.dma_start(dys[32 * q : 32 * q + 4].bitcast(I32), dy_scales[0, 4 * q : 4 * q + 4, :].bitcast(I32))
-        nc.sync.dma_start(grows[:], gate.rearrange("r (c j) -> (r c) j", j=CH)[0:P, :])
-        nc.sync.dma_start(dyw[:], dy_words[0].rearrange("p t d -> p (t d)").bitcast(I32))
+        load_dy_rows(nc.scalar, 0)
         nc.sync.dma_start(w2w[:, 0].bitcast(I32), w2t_words[0, 0].bitcast(I32))
-        load_scales(w2s, w2t_scales)
-        nc.sync.dma_start(par[:], offs2)
-        nc.sync.dma_start(w2w[:, 1].bitcast(I32), w2t_words[1, 0].bitcast(I32))
+        load_dy_rows(nc.scalar, 1)
+        load_dy_rows(nc.sync, 2)
+        nc.scalar.dma_start(dyw[:], dy_words[0].rearrange("p t d -> p (t d)").bitcast(I32))
+        load_dy_rows(nc.sync, 3)
+        load_rows(nc.sync, w2s, w2t_scales, 1)
+        load_rows(nc.sync, w2s, w2t_scales, 2)
+        load_rows(nc.sync, w2s, w2t_scales, 3)
+        with nc.allow_non_contiguous_dma(reason="one gate value a slot, slots on the partitions"):
+            nc.sync.dma_start(gcol[:], gate[0].rearrange("(c p) -> p c", p=P))
         load_words(w1w, w1t_words)
         load_scales(w1s, w1t_scales)
+        nc.sync.dma_start(w2w[:, 1].bitcast(I32), w2t_words[1, 0].bitcast(I32))
+        nc.sync.dma_start(par[:], offs2)
         load_words(wpw, wpt_words)
         load_scales(wps, wpt_scales)
-        nc.vector.memset(winx[0][:], 0.0)
-        nc.scalar.activation(winp[0][:], winx[0][:], COPY)
-        nc.gpsimd.memset(winp[1][:], 0.0)
+        nc.scalar.activation(winx[1][:], winx[0][:], COPY)
+        nc.scalar.copy(winp[0][:], winx[0][:])
 
-        gt = pst.tile([P, P], F32, name="gt", tag="tr")
-        nc.tensor.transpose(gt[:], grows[:], ident[:])
-        nc.scalar.copy(gcol[:], gt[:, 0 : S // CH])
-        nc.scalar.copy(winx[1][:], winx[0][:])
 
-        def gather_words(a, b):
-            e = a // C
-            nc.vector.tensor_copy(gw[e][:, a - e * C : b - e * C], dyw[:].bitcast(U32).indirect(tok[:, a // 16 : b // 16]))
+        def gather_scales(a, b):
+            gs = keep.tile([P, b - a], U8, name="gs%d" % a, align_bytes=64)
+            nc.vector.tensor_copy(gs[:], dys[:].indirect(tok[:, a // 16 : b // 16]))
+            return gs
 
-        def spare():
-            return psa.tile([P, BANK], F32, name="acc", tag="acc")
+        def gather_words(a, b, offset):
+            gw = words.tile([P, b - a], U32, name="gw%d" % a, align_bytes=64, offset=offset)
+            nc.vector.tensor_copy(gw[:], dyw[:].bitcast(U32).indirect(tok[:, a // 16 : b // 16]))
+            return gw
 
-        def gather_scales(e):
-            nc.vector.tensor_copy(gs[e][:], dys[:].indirect(tok[:, e * C // 16 : (e + 1) * C // 16]))
-
-        def hidden(c):
+        def hidden(c, gw, gs, parts):
             e = c * CH // C
-            own = slice(c * CH - e * C, (c + 1) * CH - e * C)
-            acc = spare()
-            nc.tensor.matmul_mx(
-                out=acc[:], lhsT=gw[e][:, own].bitcast(FP8X4), lhsT_scale=gs[e][:, own],
-                rhs=w2w[:, e, :].bitcast(FP4X4), rhs_scale=w2s[:, e, :], start=True, stop=True,
-            )
             dh = keep.tile([P, H], BF16, name="dh%d" % c)
-            dst = dh[:].rearrange("s (u p d) -> s u p d", u=2, d=2)
-            src = acc[:].rearrange("s (p u d) -> s u p d", u=2, d=2)
-            if c % 2 == 0:
-                nc.scalar.activation(dst, src, COPY, scale=gcol[:, c : c + 1])
-            else:
-                nc.vector.tensor_scalar(dst, src, gcol[:, c : c + 1], None, MULT)
+            width = H // len(parts)
+            for n, (at, on_vector) in enumerate(parts):
+                acc = banks[at][:, 0:width]
+                nc.tensor.matmul_mx(
+                    out=acc, lhsT=gw.bitcast(FP8X4), lhsT_scale=gs,
+                    rhs=w2w[:, e, 2 * width * n : 2 * width * (n + 1)].bitcast(FP4X4),
+                    rhs_scale=w2s[:, e, width * n : width * (n + 1)], start=True, stop=True,
+                )
+                dst = dh[:].rearrange("s (u p d) -> s u p d", u=2, d=2)[:, :, width // 4 * n : width // 4 * (n + 1), :]
+                src = acc.rearrange("s (p u d) -> s u p d", u=2, d=2)
+                if on_vector:
+                    nc.vector.tensor_scalar(dst, src, gcol[:, c : c + 1], None, MULT)
+                else:
+                    nc.scalar.activation(dst, src, COPY, scale=gcol[:, c : c + 1])
             return dh
 
-        def turn(c, dh):
+        def turn(dh, quads, at):
             pairs = dh[:].bitcast(F32)
-            turned = pst.tile([P, 2, CH], F32, name="turned", tag="tr")
+            turned = banks[at][:, 0 : 2 * CH].rearrange("p (u s) -> p u s", u=2)
             for u in range(2):
                 nc.tensor.transpose(turned[:, u, :], pairs[:, u * P : (u + 1) * P], ident[:])
-            quads = keep.tile([P, 4 * CH], BF16, name="quads%d" % c, align_bytes=64)
-            nc.scalar.copy(quads[:].bitcast(F32).rearrange("p (s u) -> p s u", u=2), turned[:].rearrange("p u s -> p s u"))
-            return quads
+            nc.scalar.copy(quads.bitcast(F32).rearrange("p (s u) -> p s u", u=2), turned.rearrange("p u s -> p s u"))
 
-        def quantise(c, quads):
-            cols = slice(c * CH, (c + 1) * CH)
-            nc.vector.quantize_mx(out=dqw[:, cols].bitcast(FP8X4), scales=dqs[:, cols], in_=quads[:])
-
-        def product(dst, ww, ws, m, a, b):
-            e = a // C
-            nc.tensor.matmul_mx(
-                out=dst, lhsT=ww[:, e, 2 * P * m : 2 * P * (m + 1)].bitcast(FP4X4), lhsT_scale=ws[:, e, P * m : P * (m + 1)],
-                rhs=dqw[:, a:b].bitcast(FP8X4), rhs_scale=dqs[:, a:b], start=True, stop=True,
-            )
-
-        def fresh():
-            return psy.tile([P, BANK], F32, name="y", tag="y")
-
-        def results(y, jobs):
-            at = 0
-            for side, m, a, b in jobs:
-                for lo in range(a, b, C):
-                    hi = min(b, lo + C)
-                    product(y[:, at : at + hi - lo], sides[side][0], sides[side][1], m, lo, hi)
-                    at += hi - lo
-            ys = keep.tile([P, at], F32, name="ys", tag="ys%d_%d_%d" % jobs[0][:3])
-            nc.scalar.copy(ys[:], y[:, 0:at])
-            at = 0
-            pieces = []
-            for side, m, a, b in jobs:
-                pieces.append((side, m, a, b, ys[:, at : at + b - a]))
-                at += b - a
-            return pieces
+        def quantise(a, b, quads):
+            nc.vector.quantize_mx(out=dqw[:, a:b].bitcast(FP8X4), scales=dqs[:, a:b], in_=quads)
 
         sides = ((w1w, w1s, tok, winx), (wpw, wps, par, winp))
 
-        def scatter(piece):
-            side, m, a, b, src = piece
-            nc.vector.tensor_copy(sides[side][3][m % len(sides[side][3])][:].indirect(sides[side][2][:, a // 16 : b // 16]), src)
+        def results(at, jobs):
+            y = banks[at]
+            col = 0
+            for side, m, a, b in jobs:
+                ww, ws = sides[side][:2]
+                for lo in range(a, b, C):
+                    hi = min(b, lo + C)
+                    e = lo // C
+                    nc.tensor.matmul_mx(
+                        out=y[:, col : col + hi - lo], lhsT=ww[:, e, 2 * P * m : 2 * P * (m + 1)].bitcast(FP4X4),
+                        lhsT_scale=ws[:, e, P * m : P * (m + 1)],
+                        rhs=dqw[:, lo:hi].bitcast(FP8X4), rhs_scale=dqs[:, lo:hi], start=True, stop=True,
+                    )
+                    col += hi - lo
+            ys = keep.tile([P, col], F32, name="ys", tag="ys%d_%d_%d" % jobs[0][:3])
+            nc.scalar.copy(ys[:], y[:, 0:col])
+            col = 0
+            pieces = []
+            for side, m, a, b in jobs:
+                pieces.append((side, m, a, b, ys[:, col : col + b - a]))
+                col += b - a
+            return pieces
 
-        def add_on_tensor(m, adder):
+        def scatter(piece):
+            side, m, a, b, ys = piece
+            nc.vector.tensor_copy(sides[side][3][m % 2][:].indirect(sides[side][2][:, a // 16 : b // 16]), ys)
+
+        def add_on_tensor(m):
             wx, wp = winx[m % 2], winp[m % 2]
             flipped = []
             for h in range(T // BANK):
+                adder = banks[h]
                 for j in range(BANK // P):
                     blk = slice(h * BANK + j * P, h * BANK + (j + 1) * P)
-                    dst = adder[h][:, j * P : (j + 1) * P]
+                    dst = adder[:, j * P : (j + 1) * P]
                     nc.tensor.matmul(dst, lhsT=wx[:, blk], rhs=ident[:], start=True, stop=False, is_transpose=True)
                     nc.tensor.matmul(dst, lhsT=wp[:, blk], rhs=ident[:], start=False, stop=True, is_transpose=True)
                 flipped.append(ring.tile([P, BANK], F32, name="flipped", tag="flipped"))
-                nc.scalar.copy(flipped[h][:], adder[h][:])
+                nc.scalar.copy(flipped[h][:], adder[:])
             for h in range(T // BANK):
+                back = banks[2 + h]
                 for j in range(BANK // P):
-                    nc.tensor.transpose(adder[h][:, j * P : (j + 1) * P], flipped[h][:, j * P : (j + 1) * P], ident[:])
+                    nc.tensor.transpose(back[:, j * P : (j + 1) * P], flipped[h][:, j * P : (j + 1) * P], ident[:])
                 res = ring.tile([P, BANK], F32, name="res", tag="res")
-                nc.scalar.copy(res[:], adder[h][:])
+                nc.scalar.copy(res[:], back[:])
                 nc.scalar.dma_start(out[m * P : (m + 1) * P, h * BANK : (h + 1) * BANK], res[:])
 
-        gather_scales(0)
-        gather_words(0, CH)
-        gather_words(CH, C)
-        gather_scales(1)
-        gather_words(C, S)
-        dhs = [hidden(c) for c in range(S // CH)]
-        for c in range(S // CH):
-            quantise(c, turn(c, dhs[c]))
-        todo = results(fresh(), [(0, 0, 0, C)]) + results(fresh(), [(1, 0, 0, C)])
-        adder = [spare() for h in range(T // BANK)]
-        todo += results(spare(), [(0, 0, C, S), (1, 0, C, S)])
-        for m in range(1, K // P):
-            todo += results(fresh(), [(0, m, 0, S)]) + results(spare(), [(1, m, 0, S)])
-        for piece in todo[:4]:
+        quads = keep.tile([P, 4 * S], BF16, name="quads", align_bytes=64)
+        gs = gather_scales(0, S)
+        dh0 = hidden(0, gather_words(0, CH, 0)[:], gs[:, 0:CH], [(0, False), (6, True)])
+        dh1 = hidden(1, gather_words(CH, C, 4 * CH)[:], gs[:, CH:C], [(1, True)])
+        turn(dh0, quads[:, 0 : 4 * CH], 2)
+        quantise(0, CH, quads[:, 0 : 4 * CH])
+        scatter(results(4, [(0, 0, 0, CH)])[0])
+        turn(dh1, quads[:, 4 * CH : 4 * C], 3)
+        quantise(CH, C, quads[:, 4 * CH : 4 * C])
+        for piece in results(5, [(0, 0, CH, C), (0, 1, 0, C)]):
             scatter(piece)
-        for m in range(1, K // P):
-            scatter(todo[2 * m + 2])
-            add_on_tensor(m - 1, adder)
-            scatter(todo[2 * m + 3])
+        gw1 = gather_words(C, S, 0)
+        for c in (2, 3):
+            dh = hidden(c, gw1[:, (c - 2) * CH : (c - 1) * CH], gs[:, c * CH : (c + 1) * CH], [(2 + c, False)])
+            turn(dh, quads[:, 4 * CH * c : 4 * CH * (c + 1)], c)
+        quantise(C, S, quads[:, 4 * C : 4 * S])
+        groups = [[(1, 0, 0, C)], [(0, 0, C, S)], [(1, 0, C, S), (0, 1, C, S)], [(1, 1, 0, S)]]
+        groups.extend([[(side, m, 0, S)] for m in (2, 3) for side in range(2)])
+        todo = [piece for jobs in groups for piece in results(7, jobs)]
+        for piece in todo[:3]:
+            scatter(piece)
+        add_on_tensor(0)
+        for piece in todo[3:5]:
+            scatter(piece)
+        add_on_tensor(1)
+        for piece in todo[5:7]:
+            scatter(piece)
+        add_on_tensor(2)
+        for piece in todo[7:]:
+            scatter(piece)
         m = K // P - 1
         last = keep.tile([P, T], F32, name="last")
+        edges = (0, 320, 640, 896, T)
         for h in range(4):
-            cols = slice(h * 256, (h + 1) * 256)
+            cols = slice(edges[h], edges[h + 1])
             nc.vector.tensor_tensor(last[:, cols], winx[m % 2][:, cols], winp[m % 2][:, cols], ADD)
             nc.sync.dma_start(out[m * P : (m + 1) * P, cols], last[:, cols])

@@ -73,7 +73,8 @@ def tile_moe_dub_none_kernel(
         nc.vector.memset(ident[:], 0.0)
         make_identity(nc, ident[:], nomemset=True)
         nc.vector.memset(winx[0][:], 0.0)
-        nc.gpsimd.memset(winp[1][:], 0.0)
+        nc.vector.tensor_copy(winx[1][:], winx[0][:])
+        nc.vector.tensor_copy(winp[0][:], winx[0][:])
         load_rows(nc.scalar, w2s, w2t_scales, 0)
         nc.sync.dma_start(tok[:], offs)
         load_dy_rows(nc.scalar, 0)
@@ -93,8 +94,7 @@ def tile_moe_dub_none_kernel(
         nc.sync.dma_start(par[:], offs2)
         load_words(wpw, wpt_words)
         load_scales(wps, wpt_scales)
-        nc.scalar.activation(winx[1][:], winx[0][:], COPY)
-        nc.scalar.copy(winp[0][:], winx[0][:])
+        nc.scalar.activation(winp[1][:], winx[0][:], COPY)
 
 
         def gather_scales(a, b):
@@ -217,7 +217,7 @@ def tile_moe_dub_none_kernel(
             scatter(piece)
         m = K // P - 1
         last = keep.tile([P, T], F32, name="last")
-        edges = (0, 320, 640, 896, T)
+        edges = (0, 256, 512, 768, T)
         for h in range(4):
             cols = slice(edges[h], edges[h + 1])
             nc.vector.tensor_tensor(last[:, cols], winx[m % 2][:, cols], winp[m % 2][:, cols], ADD)

@@ -48,7 +48,7 @@ def tile_moe_dub_none_kernel(
         ident = keep.tile([P, P], F32, name="ident")
         dqw = keep.tile([P, S], U32, name="dqw", align_bytes=64)
         dqs = keep.tile([P, S], U8, name="dqs", align_bytes=64)
-        winx = [keep.tile([P, T], F32, name="winx%d" % b) for b in range(2)]
+        winx = [keep.tile([P, T], F32, name="winx%d" % b, align_bytes=64) for b in range(2)]
         winp = [keep.tile([P, T], F32, name="winp%d" % b) for b in range(2)]
 
         banks = [ps.tile([P, BANK], F32, name="bank%d" % b) for b in range(8)]
@@ -73,6 +73,9 @@ def tile_moe_dub_none_kernel(
         nc.vector.memset(ident[:], 0.0)
         make_identity(nc, ident[:], nomemset=True)
         nc.vector.memset(winx[0][:], 0.0)
+        idle_words = keep.tile([P, C], U32, name="idle_words", align_bytes=64)
+        idle_scales = keep.tile([P, C], U8, name="idle_scales", align_bytes=64)
+        nc.vector.quantize_mx(out=idle_words[:].bitcast(FP8X4), scales=idle_scales[:], in_=winx[0][:].bitcast(BF16)[:, 0 : 4 * C])
         nc.vector.tensor_copy(winx[1][:], winx[0][:])
         nc.vector.tensor_copy(winp[0][:], winx[0][:])
         load_rows(nc.scalar, w2s, w2t_scales, 0)
@@ -185,6 +188,11 @@ def tile_moe_dub_none_kernel(
                 nc.scalar.copy(res[:], back[:])
                 nc.scalar.dma_start(out[m * P : (m + 1) * P, h * BANK : (h + 1) * BANK], res[:])
 
+        for n in range(6):
+            nc.tensor.matmul_mx(
+                out=banks[7][:, 0:C], lhsT=w2w[:, 0, 0 : 2 * P].bitcast(FP4X4), lhsT_scale=idle_scales[:, 0:P],
+                rhs=idle_words[:].bitcast(FP8X4), rhs_scale=idle_scales[:], start=True, stop=True,
+            )
         quads = keep.tile([P, 4 * S], BF16, name="quads", align_bytes=64)
         gs = gather_scales(0, S)
         dh0 = hidden(0, gather_words(0, CH, 0)[:], gs[:, 0:CH], [(0, False), (6, True)])

@@ -44,7 +44,7 @@ def tile_moe_dub_none_kernel(
         w2s = keep.tile([P, E, H], U8, name="w2s", align_bytes=64)
         w1s = keep.tile([P, E, K], U8, name="w1s", align_bytes=64)
         wps = keep.tile([P, E, K], U8, name="wps", align_bytes=64)
-        gcol = keep.tile([P, S // CH], F32, name="gcol")
+        gcol = [keep.tile([P, C // CH], F32, name="gcol%d" % e) for e in range(E)]
         ident = keep.tile([P, P], F32, name="ident")
         dqw = keep.tile([P, S], U32, name="dqw", align_bytes=64)
         dqs = keep.tile([P, S], U8, name="dqs", align_bytes=64)
@@ -77,7 +77,7 @@ def tile_moe_dub_none_kernel(
         idle_scales = keep.tile([P, C], U8, name="idle_scales", align_bytes=64)
         nc.vector.quantize_mx(out=idle_words[:].bitcast(FP8X4), scales=idle_scales[:], in_=winx[0][:].bitcast(BF16)[:, 0 : 4 * C])
         nc.vector.tensor_copy(winx[1][:], winx[0][:])
-        nc.vector.tensor_copy(winp[0][:], winx[0][:])
+        nc.vector.tensor_copy(winp[0][:, T // 2 : T], winx[0][:, T // 2 : T])
         load_rows(nc.scalar, w2s, w2t_scales, 0)
         nc.sync.dma_start(tok[:], offs)
         load_dy_rows(nc.scalar, 0)
@@ -90,14 +90,17 @@ def tile_moe_dub_none_kernel(
         load_rows(nc.sync, w2s, w2t_scales, 2)
         load_rows(nc.sync, w2s, w2t_scales, 3)
         with nc.allow_non_contiguous_dma(reason="one gate value a slot, slots on the partitions"):
-            nc.sync.dma_start(gcol[:], gate[0].rearrange("(c p) -> p c", p=P))
+            nc.sync.dma_start(gcol[0][:], gate[0, 0:C].rearrange("(c p) -> p c", p=P))
         load_words(w1w, w1t_words)
         load_scales(w1s, w1t_scales)
         nc.sync.dma_start(w2w[:, 1].bitcast(I32), w2t_words[1, 0].bitcast(I32))
+        with nc.allow_non_contiguous_dma(reason="one gate value a slot, slots on the partitions"):
+            nc.sync.dma_start(gcol[1][:], gate[0, C:S].rearrange("(c p) -> p c", p=P))
         nc.sync.dma_start(par[:], offs2)
         load_words(wpw, wpt_words)
         load_scales(wps, wpt_scales)
         nc.scalar.activation(winp[1][:], winx[0][:], COPY)
+        nc.scalar.copy(winp[0][:, 0 : T // 2], winx[0][:, 0 : T // 2])
 
 
         def gather_scales(a, b):
@@ -124,9 +127,9 @@ def tile_moe_dub_none_kernel(
                 dst = dh[:].rearrange("s (u p d) -> s u p d", u=2, d=2)[:, :, width // 4 * n : width // 4 * (n + 1), :]
                 src = acc.rearrange("s (p u d) -> s u p d", u=2, d=2)
                 if on_vector:
-                    nc.vector.tensor_scalar(dst, src, gcol[:, c : c + 1], None, MULT)
+                    nc.vector.tensor_scalar(dst, src, gcol[e][:, c % 2 : c % 2 + 1], None, MULT)
                 else:
-                    nc.scalar.activation(dst, src, COPY, scale=gcol[:, c : c + 1])
+                    nc.scalar.activation(dst, src, COPY, scale=gcol[e][:, c % 2 : c % 2 + 1])
             return dh
 
         def turn(dh, quads, at):
@@ -202,7 +205,7 @@ def tile_moe_dub_none_kernel(
         scatter(results(4, [(0, 0, 0, CH)])[0])
         turn(dh1, quads[:, 4 * CH : 4 * C], 3)
         quantise(CH, C, quads[:, 4 * CH : 4 * C])
-        for piece in results(5, [(0, 0, CH, C), (0, 1, 0, C)]):
+        for piece in results(5, [(0, 0, CH, C)]) + results(6, [(0, 1, 0, C)]):
             scatter(piece)
         gw1 = gather_words(C, S, 0)
         for c in (2, 3):

@@ -70,14 +70,16 @@ def tile_moe_dub_none_kernel(
             queue.dma_start(dys[32 * q : 32 * q + 4].bitcast(I32), dy_scales[0, 4 * q : 4 * q + 4, :].bitcast(I32))
 
         nc.vector.memset(dys[:].bitcast(I32), 0)
+        zero = keep.tile([P, 8], F32, name="zero")
+        nc.vector.memset(zero[:], 0.0)
         nc.vector.memset(ident[:], 0.0)
         make_identity(nc, ident[:], nomemset=True)
-        nc.vector.memset(winx[0][:], 0.0)
+        zeros = zero[:, 0:1].to_broadcast([P, T])
+        nc.vector.tensor_copy(winx[0][:], zeros)
+        nc.vector.tensor_copy(winx[1][:], zeros)
         idle_words = keep.tile([P, C], U32, name="idle_words", align_bytes=64)
         idle_scales = keep.tile([P, C], U8, name="idle_scales", align_bytes=64)
         nc.vector.quantize_mx(out=idle_words[:].bitcast(FP8X4), scales=idle_scales[:], in_=winx[0][:].bitcast(BF16)[:, 0 : 4 * C])
-        nc.vector.tensor_copy(winx[1][:], winx[0][:])
-        nc.vector.tensor_copy(winp[0][:, T // 2 : T], winx[0][:, T // 2 : T])
         load_rows(nc.scalar, w2s, w2t_scales, 0)
         nc.sync.dma_start(tok[:], offs)
         load_dy_rows(nc.scalar, 0)
@@ -99,8 +101,8 @@ def tile_moe_dub_none_kernel(
         nc.sync.dma_start(par[:], offs2)
         load_words(wpw, wpt_words)
         load_scales(wps, wpt_scales)
-        nc.scalar.activation(winp[1][:], winx[0][:], COPY)
-        nc.scalar.copy(winp[0][:, 0 : T // 2], winx[0][:, 0 : T // 2])
+        nc.scalar.activation(winp[0][:], zeros, COPY)
+        nc.scalar.copy(winp[1][:], zeros)
 
 
         def gather_scales(a, b):
@@ -205,7 +207,7 @@ def tile_moe_dub_none_kernel(
         scatter(results(4, [(0, 0, 0, CH)])[0])
         turn(dh1, quads[:, 4 * CH : 4 * C], 3)
         quantise(CH, C, quads[:, 4 * CH : 4 * C])
-        for piece in results(5, [(0, 0, CH, C)]) + results(6, [(0, 1, 0, C)]):
+        for piece in results(6, [(0, 1, 0, C)]) + results(5, [(0, 0, CH, C)]):
             scatter(piece)
         gw1 = gather_words(C, S, 0)
         for c in (2, 3):

@@ -77,9 +77,6 @@ def tile_moe_dub_none_kernel(
         zeros = zero[:, 0:1].to_broadcast([P, T])
         nc.vector.tensor_copy(winx[0][:], zeros)
         nc.vector.tensor_copy(winx[1][:], zeros)
-        idle_words = keep.tile([P, C], U32, name="idle_words", align_bytes=64)
-        idle_scales = keep.tile([P, C], U8, name="idle_scales", align_bytes=64)
-        nc.vector.quantize_mx(out=idle_words[:].bitcast(FP8X4), scales=idle_scales[:], in_=winx[0][:].bitcast(BF16)[:, 0 : 4 * C])
         load_rows(nc.scalar, w2s, w2t_scales, 0)
         nc.sync.dma_start(tok[:], offs)
         load_dy_rows(nc.scalar, 0)
@@ -193,11 +190,6 @@ def tile_moe_dub_none_kernel(
                 nc.scalar.copy(res[:], back[:])
                 nc.scalar.dma_start(out[m * P : (m + 1) * P, h * BANK : (h + 1) * BANK], res[:])
 
-        for n in range(6):
-            nc.tensor.matmul_mx(
-                out=banks[7][:, 0:C], lhsT=w2w[:, 0, 0 : 2 * P].bitcast(FP4X4), lhsT_scale=idle_scales[:, 0:P],
-                rhs=idle_words[:].bitcast(FP8X4), rhs_scale=idle_scales[:], start=True, stop=True,
-            )
         quads = keep.tile([P, 4 * S], BF16, name="quads", align_bytes=64)
         gs = gather_scales(0, S)
         dh0 = hidden(0, gather_words(0, CH, 0)[:], gs[:, 0:CH], [(0, False), (6, True)])

@@ -66,6 +66,15 @@ def tile_moe_dub_none_kernel(
             for q in range(4):
                 load_rows(nc.sync, tile, scales, q)
 
+        def load_gate(e):
+            third = (S + 1) // 3
+            count = 3 * (P - 1) + 1
+            start = min(e * C, P * S - count * third)
+            lines = gate.rearrange("r s -> (r s)")[start : start + count * third].rearrange("(n x) -> n x", x=third)
+            picked = lines[0:count:3, e * C - start : third : CH]
+            with nc.allow_non_contiguous_dma(reason="one gate value a slot, slots on the partitions"):
+                nc.sync.dma_start(gcol[e][:], picked)
+
         def load_dy_rows(queue, q):
             queue.dma_start(dys[32 * q : 32 * q + 4].bitcast(I32), dy_scales[0, 4 * q : 4 * q + 4, :].bitcast(I32))
 
@@ -88,13 +97,11 @@ def tile_moe_dub_none_kernel(
         load_rows(nc.sync, w2s, w2t_scales, 1)
         load_rows(nc.sync, w2s, w2t_scales, 2)
         load_rows(nc.sync, w2s, w2t_scales, 3)
-        with nc.allow_non_contiguous_dma(reason="one gate value a slot, slots on the partitions"):
-            nc.sync.dma_start(gcol[0][:], gate[0, 0:C].rearrange("(c p) -> p c", p=P))
+        load_gate(0)
         load_words(w1w, w1t_words)
         load_scales(w1s, w1t_scales)
         nc.sync.dma_start(w2w[:, 1].bitcast(I32), w2t_words[1, 0].bitcast(I32))
-        with nc.allow_non_contiguous_dma(reason="one gate value a slot, slots on the partitions"):
-            nc.sync.dma_start(gcol[1][:], gate[0, C:S].rearrange("(c p) -> p c", p=P))
+        load_gate(1)
         nc.sync.dma_start(par[:], offs2)
         load_words(wpw, wpt_words)
         load_scales(wps, wpt_scales)

@@ -30,8 +30,6 @@ def tile_moe_dub_none_kernel(
     nc = tc.nc
     with ExitStack() as ctx:
         keep = ctx.enter_context(tc.tile_pool(name="keep", bufs=1))
-        ring = ctx.enter_context(tc.tile_pool(name="ring", bufs=2))
-        words = ctx.enter_context(tc.tile_pool(name="words", bufs=1))
         ps = ctx.enter_context(tc.psum_pool(name="ps", bufs=1))
 
         tok = keep.tile([P, S // 16], U16, name="tok")
@@ -46,15 +44,14 @@ def tile_moe_dub_none_kernel(
         wps = keep.tile([P, E, K], U8, name="wps", align_bytes=64)
         gcol = [keep.tile([P, C // CH], F32, name="gcol%d" % e) for e in range(E)]
         ident = keep.tile([P, P], F32, name="ident")
+        zero = keep.tile([P, 8], F32, name="zero")
+        gs = keep.tile([P, S], U8, name="gs", align_bytes=64)
+        quads = keep.tile([P, 4 * S], BF16, name="quads", align_bytes=64)
         dqw = keep.tile([P, S], U32, name="dqw", align_bytes=64)
         dqs = keep.tile([P, S], U8, name="dqs", align_bytes=64)
-        winx = [keep.tile([P, T], F32, name="winx%d" % b, align_bytes=64) for b in range(2)]
-        winp = [keep.tile([P, T], F32, name="winp%d" % b) for b in range(2)]
-
+        wins = [[keep.tile([P, T], F32, name="win%d_%d" % (side, b)) for b in range(3)] for side in range(2)]
+        sums = [keep.tile([P, T], F32, name="sum%d" % m) for m in range(K // P)]
         banks = [ps.tile([P, BANK], F32, name="bank%d" % b) for b in range(8)]
-
-        def load_words(tile, words):
-            nc.sync.dma_start(tile[:].bitcast(I32), words[:, 0].rearrange("e p n -> p e n").bitcast(I32))
 
         def load_rows(queue, tile, scales, q):
             queue.dma_start(
@@ -62,71 +59,58 @@ def tile_moe_dub_none_kernel(
                 scales[:, 0, 4 * q : 4 * q + 4, :].rearrange("e r n -> r e n").bitcast(I32),
             )
 
-        def load_scales(tile, scales):
+        def load_matrix(wtile, stile, words, scales):
+            nc.sync.dma_start(wtile[:].bitcast(I32), words[:, 0].rearrange("e p n -> p e n").bitcast(I32))
             for q in range(4):
-                load_rows(nc.sync, tile, scales, q)
+                load_rows(nc.sync, stile, scales, q)
 
         def load_gate(e):
-            third = (S + 1) // 3
-            count = 3 * (P - 1) + 1
-            start = min(e * C, P * S - count * third)
-            lines = gate.rearrange("r s -> (r s)")[start : start + count * third].rearrange("(n x) -> n x", x=third)
-            picked = lines[0:count:3, e * C - start : third : CH]
             with nc.allow_non_contiguous_dma(reason="one gate value a slot, slots on the partitions"):
-                nc.sync.dma_start(gcol[e][:], picked)
+                nc.sync.dma_start(gcol[e][:], gate[0, e * C : (e + 1) * C].rearrange("(c p) -> p c", p=P))
 
         def load_dy_rows(queue, q):
             queue.dma_start(dys[32 * q : 32 * q + 4].bitcast(I32), dy_scales[0, 4 * q : 4 * q + 4, :].bitcast(I32))
 
         nc.vector.memset(dys[:].bitcast(I32), 0)
-        zero = keep.tile([P, 8], F32, name="zero")
         nc.vector.memset(zero[:], 0.0)
         nc.vector.memset(ident[:], 0.0)
         make_identity(nc, ident[:], nomemset=True)
         zeros = zero[:, 0:1].to_broadcast([P, T])
-        nc.vector.tensor_copy(winx[0][:], zeros)
-        nc.vector.tensor_copy(winx[1][:], zeros)
+        nc.vector.tensor_copy(wins[0][0][:], zeros)
+        nc.vector.tensor_copy(wins[0][1][:], zeros)
         load_rows(nc.scalar, w2s, w2t_scales, 0)
         nc.sync.dma_start(tok[:], offs)
         load_dy_rows(nc.scalar, 0)
-        nc.sync.dma_start(w2w[:, 0].bitcast(I32), w2t_words[0, 0].bitcast(I32))
+        nc.sync.dma_start(w2w[:].bitcast(I32), w2t_words[:, 0].rearrange("e p n -> p e n").bitcast(I32))
         load_dy_rows(nc.scalar, 1)
         load_dy_rows(nc.sync, 2)
         nc.scalar.dma_start(dyw[:], dy_words[0].rearrange("p t d -> p (t d)").bitcast(I32))
         load_dy_rows(nc.sync, 3)
-        load_rows(nc.sync, w2s, w2t_scales, 1)
-        load_rows(nc.sync, w2s, w2t_scales, 2)
-        load_rows(nc.sync, w2s, w2t_scales, 3)
+        for q in range(1, 4):
+            load_rows(nc.sync, w2s, w2t_scales, q)
         load_gate(0)
-        load_words(w1w, w1t_words)
-        load_scales(w1s, w1t_scales)
-        nc.sync.dma_start(w2w[:, 1].bitcast(I32), w2t_words[1, 0].bitcast(I32))
         load_gate(1)
+        load_matrix(w1w, w1s, w1t_words, w1t_scales)
         nc.sync.dma_start(par[:], offs2)
-        load_words(wpw, wpt_words)
-        load_scales(wps, wpt_scales)
-        nc.scalar.activation(winp[0][:], zeros, COPY)
-        nc.scalar.copy(winp[1][:], zeros)
+        load_matrix(wpw, wps, wpt_words, wpt_scales)
+        nc.scalar.copy(wins[1][0][:], zeros)
+        nc.scalar.copy(wins[1][1][:], zeros)
+        nc.gpsimd.memset(wins[0][2][:], 0.0)
+        nc.gpsimd.memset(wins[1][2][:], 0.0)
 
-
-        def gather_scales(a, b):
-            gs = keep.tile([P, b - a], U8, name="gs%d" % a, align_bytes=64)
-            nc.vector.tensor_copy(gs[:], dys[:].indirect(tok[:, a // 16 : b // 16]))
-            return gs
-
-        def gather_words(a, b, offset):
-            gw = words.tile([P, b - a], U32, name="gw%d" % a, align_bytes=64, offset=offset)
+        def gather_words(a, b):
+            gw = keep.tile([P, b - a], U32, name="gw%d" % a, align_bytes=64)
             nc.vector.tensor_copy(gw[:], dyw[:].bitcast(U32).indirect(tok[:, a // 16 : b // 16]))
             return gw
 
-        def hidden(c, gw, gs, parts):
+        def hidden(c, gw, parts):
             e = c * CH // C
             dh = keep.tile([P, H], BF16, name="dh%d" % c)
             width = H // len(parts)
             for n, (at, on_vector) in enumerate(parts):
                 acc = banks[at][:, 0:width]
                 nc.tensor.matmul_mx(
-                    out=acc, lhsT=gw.bitcast(FP8X4), lhsT_scale=gs,
+                    out=acc, lhsT=gw.bitcast(FP8X4), lhsT_scale=gs[:, c * CH : (c + 1) * CH],
                     rhs=w2w[:, e, 2 * width * n : 2 * width * (n + 1)].bitcast(FP4X4),
                     rhs_scale=w2s[:, e, width * n : width * (n + 1)], start=True, stop=True,
                 )
@@ -138,99 +122,88 @@ def tile_moe_dub_none_kernel(
                     nc.scalar.activation(dst, src, COPY, scale=gcol[e][:, c % 2 : c % 2 + 1])
             return dh
 
-        def turn(dh, quads, at):
+        def turn(dh, c, at, on_vector):
             pairs = dh[:].bitcast(F32)
             turned = banks[at][:, 0 : 2 * CH].rearrange("p (u s) -> p u s", u=2)
             for u in range(2):
                 nc.tensor.transpose(turned[:, u, :], pairs[:, u * P : (u + 1) * P], ident[:])
-            nc.scalar.copy(quads.bitcast(F32).rearrange("p (s u) -> p s u", u=2), turned.rearrange("p u s -> p s u"))
+            dst = quads[:, 4 * CH * c : 4 * CH * (c + 1)].bitcast(F32).rearrange("p (s u) -> p s u", u=2)
+            if on_vector:
+                nc.vector.tensor_copy(dst, turned.rearrange("p u s -> p s u"))
+            else:
+                nc.scalar.copy(dst, turned.rearrange("p u s -> p s u"))
 
-        def quantise(a, b, quads):
-            nc.vector.quantize_mx(out=dqw[:, a:b].bitcast(FP8X4), scales=dqs[:, a:b], in_=quads)
+        def quantise(a, b):
+            nc.vector.quantize_mx(out=dqw[:, a:b].bitcast(FP8X4), scales=dqs[:, a:b], in_=quads[:, 4 * a : 4 * b])
 
-        sides = ((w1w, w1s, tok, winx), (wpw, wps, par, winp))
+        sides = ((w1w, w1s, tok), (wpw, wps, par))
 
-        def results(at, jobs):
+        def product(eng, at, jobs):
             y = banks[at]
-            col = 0
-            for side, m, a, b in jobs:
+            for n, (side, m, e) in enumerate(jobs):
                 ww, ws = sides[side][:2]
-                for lo in range(a, b, C):
-                    hi = min(b, lo + C)
-                    e = lo // C
-                    nc.tensor.matmul_mx(
-                        out=y[:, col : col + hi - lo], lhsT=ww[:, e, 2 * P * m : 2 * P * (m + 1)].bitcast(FP4X4),
-                        lhsT_scale=ws[:, e, P * m : P * (m + 1)],
-                        rhs=dqw[:, lo:hi].bitcast(FP8X4), rhs_scale=dqs[:, lo:hi], start=True, stop=True,
-                    )
-                    col += hi - lo
-            ys = keep.tile([P, col], F32, name="ys", tag="ys%d_%d_%d" % jobs[0][:3])
-            nc.scalar.copy(ys[:], y[:, 0:col])
-            col = 0
-            pieces = []
-            for side, m, a, b in jobs:
-                pieces.append((side, m, a, b, ys[:, col : col + b - a]))
-                col += b - a
-            return pieces
+                nc.tensor.matmul_mx(
+                    out=y[:, n * C : (n + 1) * C], lhsT=ww[:, e, 2 * P * m : 2 * P * (m + 1)].bitcast(FP4X4),
+                    lhsT_scale=ws[:, e, P * m : P * (m + 1)],
+                    rhs=dqw[:, e * C : (e + 1) * C].bitcast(FP8X4), rhs_scale=dqs[:, e * C : (e + 1) * C],
+                    start=True, stop=True,
+                )
+            width = len(jobs) * C
+            ys = keep.tile([P, width], F32, name="ys%d_%d_%d" % jobs[0])
+            if eng == 0:
+                nc.vector.tensor_copy(ys[:], y[:, 0:width])
+            else:
+                nc.scalar.copy(ys[:], y[:, 0:width])
+            return ys
 
-        def scatter(piece):
-            side, m, a, b, ys = piece
-            nc.vector.tensor_copy(sides[side][3][m % 2][:].indirect(sides[side][2][:, a // 16 : b // 16]), ys)
+        def scatter(eng, side, m, a, b, ys):
+            target = wins[side][m % 3][:].indirect(sides[side][2][:, a // 16 : b // 16])
+            if eng == 0:
+                nc.vector.tensor_copy(target, ys)
+            else:
+                nc.scalar.activation(target, ys, COPY)
 
-        def add_on_tensor(m):
-            wx, wp = winx[m % 2], winp[m % 2]
-            flipped = []
-            for h in range(T // BANK):
-                adder = banks[h]
-                for j in range(BANK // P):
-                    blk = slice(h * BANK + j * P, h * BANK + (j + 1) * P)
-                    dst = adder[:, j * P : (j + 1) * P]
-                    nc.tensor.matmul(dst, lhsT=wx[:, blk], rhs=ident[:], start=True, stop=False, is_transpose=True)
-                    nc.tensor.matmul(dst, lhsT=wp[:, blk], rhs=ident[:], start=False, stop=True, is_transpose=True)
-                flipped.append(ring.tile([P, BANK], F32, name="flipped", tag="flipped"))
-                nc.scalar.copy(flipped[h][:], adder[:])
-            for h in range(T // BANK):
-                back = banks[2 + h]
-                for j in range(BANK // P):
-                    nc.tensor.transpose(back[:, j * P : (j + 1) * P], flipped[h][:, j * P : (j + 1) * P], ident[:])
-                res = ring.tile([P, BANK], F32, name="res", tag="res")
-                nc.scalar.copy(res[:], back[:])
-                nc.scalar.dma_start(out[m * P : (m + 1) * P, h * BANK : (h + 1) * BANK], res[:])
+        def add_early(m):
+            nc.gpsimd.tensor_tensor(sums[m][:], wins[0][m % 3][:], wins[1][m % 3][:], ADD)
+            nc.sync.dma_start(out[m * P : (m + 1) * P, :], sums[m][:])
 
-        quads = keep.tile([P, 4 * S], BF16, name="quads", align_bytes=64)
-        gs = gather_scales(0, S)
-        dh0 = hidden(0, gather_words(0, CH, 0)[:], gs[:, 0:CH], [(0, False), (6, True)])
-        dh1 = hidden(1, gather_words(CH, C, 4 * CH)[:], gs[:, CH:C], [(1, True)])
-        turn(dh0, quads[:, 0 : 4 * CH], 2)
-        quantise(0, CH, quads[:, 0 : 4 * CH])
-        scatter(results(4, [(0, 0, 0, CH)])[0])
-        turn(dh1, quads[:, 4 * CH : 4 * C], 3)
-        quantise(CH, C, quads[:, 4 * CH : 4 * C])
-        for piece in results(6, [(0, 1, 0, C)]) + results(5, [(0, 0, CH, C)]):
-            scatter(piece)
-        gw1 = gather_words(C, S, 0)
-        for c in (2, 3):
-            dh = hidden(c, gw1[:, (c - 2) * CH : (c - 1) * CH], gs[:, c * CH : (c + 1) * CH], [(2 + c, False)])
-            turn(dh, quads[:, 4 * CH * c : 4 * CH * (c + 1)], c)
-        quantise(C, S, quads[:, 4 * C : 4 * S])
-        groups = [[(1, 0, 0, C)], [(0, 0, C, S)], [(1, 0, C, S), (0, 1, C, S)], [(1, 1, 0, S)]]
-        groups.extend([[(side, m, 0, S)] for m in (2, 3) for side in range(2)])
-        todo = [piece for jobs in groups for piece in results(7, jobs)]
-        for piece in todo[:3]:
-            scatter(piece)
-        add_on_tensor(0)
-        for piece in todo[3:5]:
-            scatter(piece)
-        add_on_tensor(1)
-        for piece in todo[5:7]:
-            scatter(piece)
-        add_on_tensor(2)
-        for piece in todo[7:]:
-            scatter(piece)
+        nc.vector.tensor_copy(gs[:], dys[:].indirect(tok[:]))
+        gw0 = gather_words(0, CH)
+        gw1 = gather_words(CH, C)
+        gw2 = gather_words(C, S)
+        dh0 = hidden(0, gw0[:], [(0, False), (1, False)])
+        dh1 = hidden(1, gw1[:], [(2, False), (3, True)])
+        dh2 = hidden(2, gw2[:, 0:CH], [(4, True)])
+        dh3 = hidden(3, gw2[:, CH:C], [(5, False)])
+        turn(dh0, 0, 6, False)
+        turn(dh1, 1, 7, True)
+        quantise(0, C)
+        turn(dh2, 2, 0, False)
+        turn(dh3, 3, 1, False)
+        first = [product(eng, 4 + 2 * eng, [(0, eng, 0)]) for eng in range(2)]
+        quantise(C, S)
+        scatter(0, 0, 0, 0, C, first[0][:])
+        second = [product(eng, 5 + 2 * eng, [(1, eng, 0)]) for eng in range(2)]
+        scatter(1, 0, 1, 0, C, first[1][:])
+        third = [product(eng, 4 + 2 * eng, [(0, eng, 1), (1, eng, 1)]) for eng in range(2)]
+        for eng in range(2):
+            scatter(eng, 1, eng, 0, C, second[eng][:])
+            scatter(eng, 0, eng, C, S, third[eng][:, 0:C])
+        fourth = [product(eng, 5 + 2 * eng, [(eng, 2, 0), (eng, 2, 1)]) for eng in range(2)]
+        for eng in range(2):
+            scatter(eng, 1, eng, C, S, third[eng][:, C:S])
+        add_early(0)
+        add_early(1)
+        scatter(1, 1, 2, 0, C, fourth[1][:, 0:C])
+        fifth = [product(eng, 4 + 2 * eng, [(eng, 3, 0), (eng, 3, 1)]) for eng in range(2)]
+        scatter(0, 0, 2, 0, S, fourth[0][:])
+        scatter(1, 1, 2, C, S, fourth[1][:, C:S])
+        add_early(2)
+        scatter(0, 0, 3, 0, S, fifth[0][:])
+        scatter(1, 1, 3, 0, C, fifth[1][:, 0:C])
+        scatter(1, 1, 3, C, S, fifth[1][:, C:S])
         m = K // P - 1
-        last = keep.tile([P, T], F32, name="last")
-        edges = (0, 256, 512, 768, T)
         for h in range(4):
-            cols = slice(edges[h], edges[h + 1])
-            nc.vector.tensor_tensor(last[:, cols], winx[m % 2][:, cols], winp[m % 2][:, cols], ADD)
-            nc.sync.dma_start(out[m * P : (m + 1) * P, cols], last[:, cols])
+            cols = slice(h * T // 4, (h + 1) * T // 4)
+            nc.vector.tensor_tensor(sums[m][:, cols], wins[0][m % 3][:, cols], wins[1][m % 3][:, cols], ADD)
+            nc.sync.dma_start(out[m * P : (m + 1) * P, cols], sums[m][:, cols])

@@ -1,7 +1,6 @@
 from contextlib import ExitStack
 
 import concourse.mybir as mybir
-from concourse.masks import make_identity
 
 K, T, E, C, H, N = 512, 1024, 2, 256, 512, 512
 S = E * C
@@ -30,26 +29,28 @@ def tile_moe_dub_none_kernel(
     nc = tc.nc
     with ExitStack() as ctx:
         keep = ctx.enter_context(tc.tile_pool(name="keep", bufs=1))
+        late = ctx.enter_context(tc.tile_pool(name="late", bufs=1))
         ps = ctx.enter_context(tc.psum_pool(name="ps", bufs=1))
 
         tok = keep.tile([P, S // 16], U16, name="tok")
         par = keep.tile([P, S // 16], U16, name="par")
         dyw = keep.tile([P, T], I32, name="dyw", align_bytes=64)
         dys = keep.tile([P, T], U8, name="dys", align_bytes=64)
-        w2w = keep.tile([P, E, 2 * H], U8, name="w2w", align_bytes=64)
+        w2w = [keep.tile([P, 2 * H], U8, name="w2w%d" % e, align_bytes=64) for e in range(E)]
+        w2p = [keep.tile([P, 2 * H], U8, name="w2p%d" % e, align_bytes=64) for e in range(E)]
+        w2q = [keep.tile([P, H], U8, name="w2q%d" % e, align_bytes=64) for e in range(E)]
         w1w = keep.tile([P, E, 2 * K], U8, name="w1w", align_bytes=64)
         wpw = keep.tile([P, E, 2 * K], U8, name="wpw", align_bytes=64)
-        w2s = keep.tile([P, E, H], U8, name="w2s", align_bytes=64)
+        w2s = late.tile([P, E, H], U8, name="w2s", align_bytes=64, offset=8 * T)
         w1s = keep.tile([P, E, K], U8, name="w1s", align_bytes=64)
         wps = keep.tile([P, E, K], U8, name="wps", align_bytes=64)
-        gcol = [keep.tile([P, C // CH], F32, name="gcol%d" % e) for e in range(E)]
-        ident = keep.tile([P, P], F32, name="ident")
+        gates = keep.tile([P, S], F32, name="gates")
         zero = keep.tile([P, 8], F32, name="zero")
         gs = keep.tile([P, S], U8, name="gs", align_bytes=64)
-        quads = keep.tile([P, 4 * S], BF16, name="quads", align_bytes=64)
+        quads = late.tile([P, 4 * S], BF16, name="quads", align_bytes=64, offset=2 * T)
         dqw = keep.tile([P, S], U32, name="dqw", align_bytes=64)
         dqs = keep.tile([P, S], U8, name="dqs", align_bytes=64)
-        wins = [[keep.tile([P, T], F32, name="win%d_%d" % (side, b)) for b in range(3)] for side in range(2)]
+        wins = [[keep.tile([P, T], F32, name="win%d_%d" % (side, b)) for b in range(2 - side)] for side in range(2)]
         sums = [keep.tile([P, T], F32, name="sum%d" % m) for m in range(K // P)]
         banks = [ps.tile([P, BANK], F32, name="bank%d" % b) for b in range(8)]
 
@@ -64,96 +65,84 @@ def tile_moe_dub_none_kernel(
             for q in range(4):
                 load_rows(nc.sync, stile, scales, q)
 
-        def load_gate(e):
-            with nc.allow_non_contiguous_dma(reason="one gate value a slot, slots on the partitions"):
-                nc.sync.dma_start(gcol[e][:], gate[0, e * C : (e + 1) * C].rearrange("(c p) -> p c", p=P))
-
         def load_dy_rows(queue, q):
             queue.dma_start(dys[32 * q : 32 * q + 4].bitcast(I32), dy_scales[0, 4 * q : 4 * q + 4, :].bitcast(I32))
 
-        nc.vector.memset(dys[:].bitcast(I32), 0)
+        nc.gpsimd.memset(dys[:].bitcast(I32), 0)
+        nc.vector.memset(w2s[:].bitcast(I32), 0)
         nc.vector.memset(zero[:], 0.0)
-        nc.vector.memset(ident[:], 0.0)
-        make_identity(nc, ident[:], nomemset=True)
         zeros = zero[:, 0:1].to_broadcast([P, T])
         nc.vector.tensor_copy(wins[0][0][:], zeros)
         nc.vector.tensor_copy(wins[0][1][:], zeros)
-        load_rows(nc.scalar, w2s, w2t_scales, 0)
+        nc.vector.tensor_copy(wins[1][0][:], zeros)
+        nc.scalar.dma_start(w2w[0][:].bitcast(I32), w2t_words[0, 0].bitcast(I32))
         nc.sync.dma_start(tok[:], offs)
         load_dy_rows(nc.scalar, 0)
-        nc.sync.dma_start(w2w[:].bitcast(I32), w2t_words[:, 0].rearrange("e p n -> p e n").bitcast(I32))
-        load_dy_rows(nc.scalar, 1)
         load_dy_rows(nc.sync, 2)
-        nc.scalar.dma_start(dyw[:], dy_words[0].rearrange("p t d -> p (t d)").bitcast(I32))
+        load_dy_rows(nc.scalar, 1)
         load_dy_rows(nc.sync, 3)
-        for q in range(1, 4):
+        nc.scalar.dma_start(dyw[:], dy_words[0].rearrange("p t d -> p (t d)").bitcast(I32))
+        for q in range(4):
             load_rows(nc.sync, w2s, w2t_scales, q)
-        load_gate(0)
-        load_gate(1)
+        nc.sync.dma_start(w2w[1][:].bitcast(I32), w2t_words[1, 0].bitcast(I32))
+        nc.sync.dma_start(gates[:], gate)
         load_matrix(w1w, w1s, w1t_words, w1t_scales)
         nc.sync.dma_start(par[:], offs2)
         load_matrix(wpw, wps, wpt_words, wpt_scales)
-        nc.scalar.copy(wins[1][0][:], zeros)
-        nc.scalar.copy(wins[1][1][:], zeros)
-        nc.gpsimd.memset(wins[0][2][:], 0.0)
-        nc.gpsimd.memset(wins[1][2][:], 0.0)
 
-        def gather_words(a, b):
-            gw = keep.tile([P, b - a], U32, name="gw%d" % a, align_bytes=64)
+        def permute(e):
+            nc.scalar.copy(
+                w2p[e][:].bitcast(U16).rearrange("p (t m) -> p t m", t=4),
+                w2w[e][:].bitcast(U16).rearrange("p (m t) -> p t m", t=4),
+            )
+            nc.vector.tensor_copy(
+                w2q[e][:].rearrange("p (t m) -> p t m", t=4), w2s[:, e, :].rearrange("p (m t) -> p t m", t=4)
+            )
+
+        def gather_words(a, b, offset):
+            gw = late.tile([P, b - a], U32, name="gw%d" % a, align_bytes=64, offset=offset)
             nc.vector.tensor_copy(gw[:], dyw[:].bitcast(U32).indirect(tok[:, a // 16 : b // 16]))
             return gw
 
-        def hidden(c, gw, parts):
+        def hidden(c, gw):
             e = c * CH // C
-            dh = keep.tile([P, H], BF16, name="dh%d" % c)
-            width = H // len(parts)
-            for n, (at, on_vector) in enumerate(parts):
-                acc = banks[at][:, 0:width]
+            acc = banks[c][:].rearrange("p (t s) -> p t s", t=4)
+            for t in range(4):
                 nc.tensor.matmul_mx(
-                    out=acc, lhsT=gw.bitcast(FP8X4), lhsT_scale=gs[:, c * CH : (c + 1) * CH],
-                    rhs=w2w[:, e, 2 * width * n : 2 * width * (n + 1)].bitcast(FP4X4),
-                    rhs_scale=w2s[:, e, width * n : width * (n + 1)], start=True, stop=True,
+                    out=acc[:, t, :], lhsT=w2p[e][:, 2 * P * t : 2 * P * (t + 1)].bitcast(FP4X4),
+                    lhsT_scale=w2q[e][:, P * t : P * (t + 1)],
+                    rhs=gw.bitcast(FP8X4), rhs_scale=gs[:, c * CH : (c + 1) * CH], start=True, stop=True,
                 )
-                dst = dh[:].rearrange("s (u p d) -> s u p d", u=2, d=2)[:, :, width // 4 * n : width // 4 * (n + 1), :]
-                src = acc.rearrange("s (p u d) -> s u p d", u=2, d=2)
-                if on_vector:
-                    nc.vector.tensor_scalar(dst, src, gcol[e][:, c % 2 : c % 2 + 1], None, MULT)
-                else:
-                    nc.scalar.activation(dst, src, COPY, scale=gcol[e][:, c % 2 : c % 2 + 1])
-            return dh
-
-        def turn(dh, c, at, on_vector):
-            pairs = dh[:].bitcast(F32)
-            turned = banks[at][:, 0 : 2 * CH].rearrange("p (u s) -> p u s", u=2)
-            for u in range(2):
-                nc.tensor.transpose(turned[:, u, :], pairs[:, u * P : (u + 1) * P], ident[:])
-            dst = quads[:, 4 * CH * c : 4 * CH * (c + 1)].bitcast(F32).rearrange("p (s u) -> p s u", u=2)
-            if on_vector:
-                nc.vector.tensor_copy(dst, turned.rearrange("p u s -> p s u"))
-            else:
-                nc.scalar.copy(dst, turned.rearrange("p u s -> p s u"))
+            g = gates[:, c * CH : (c + 1) * CH].unsqueeze(2).to_broadcast([P, CH, 4])
+            dst = quads[:, 4 * CH * c : 4 * CH * (c + 1)].rearrange("p (s t) -> p s t", t=4)
+            nc.vector.tensor_tensor(dst, acc.rearrange("p t s -> p s t"), g, MULT)
 
         def quantise(a, b):
             nc.vector.quantize_mx(out=dqw[:, a:b].bitcast(FP8X4), scales=dqs[:, a:b], in_=quads[:, 4 * a : 4 * b])
 
         sides = ((w1w, w1s, tok), (wpw, wps, par))
 
-        def product(eng, at, jobs):
+        def product(eng, at, jobs, offset=None):
             y = banks[at]
-            for n, (side, m, e) in enumerate(jobs):
+            col = 0
+            for side, m, a, b in jobs:
                 ww, ws = sides[side][:2]
+                e = a // C
                 nc.tensor.matmul_mx(
-                    out=y[:, n * C : (n + 1) * C], lhsT=ww[:, e, 2 * P * m : 2 * P * (m + 1)].bitcast(FP4X4),
+                    out=y[:, col : col + b - a], lhsT=ww[:, e, 2 * P * m : 2 * P * (m + 1)].bitcast(FP4X4),
                     lhsT_scale=ws[:, e, P * m : P * (m + 1)],
-                    rhs=dqw[:, e * C : (e + 1) * C].bitcast(FP8X4), rhs_scale=dqs[:, e * C : (e + 1) * C],
-                    start=True, stop=True,
+                    rhs=dqw[:, a:b].bitcast(FP8X4), rhs_scale=dqs[:, a:b], start=True, stop=True,
                 )
-            width = len(jobs) * C
-            ys = keep.tile([P, width], F32, name="ys%d_%d_%d" % jobs[0])
-            if eng == 0:
-                nc.vector.tensor_copy(ys[:], y[:, 0:width])
+                col += b - a
+            name = "ys%d_%d_%d" % jobs[0][:3]
+            if offset is None:
+                ys = keep.tile([P, col], F32, name=name)
             else:
-                nc.scalar.copy(ys[:], y[:, 0:width])
+                ys = late.tile([P, col], F32, name=name, align_bytes=64, offset=offset)
+            if eng == 0:
+                nc.vector.tensor_copy(ys[:], y[:, 0:col])
+            else:
+                nc.scalar.copy(ys[:], y[:, 0:col])
             return ys
 
         def scatter(eng, side, m, a, b, ys):
@@ -168,40 +157,52 @@ def tile_moe_dub_none_kernel(
             nc.sync.dma_start(out[m * P : (m + 1) * P, :], sums[m][:])
 
         nc.vector.tensor_copy(gs[:], dys[:].indirect(tok[:]))
-        gw0 = gather_words(0, CH)
-        gw1 = gather_words(CH, C)
-        gw2 = gather_words(C, S)
-        dh0 = hidden(0, gw0[:], [(0, False), (1, False)])
-        dh1 = hidden(1, gw1[:], [(2, False), (3, True)])
-        dh2 = hidden(2, gw2[:, 0:CH], [(4, True)])
-        dh3 = hidden(3, gw2[:, CH:C], [(5, False)])
-        turn(dh0, 0, 6, False)
-        turn(dh1, 1, 7, True)
-        quantise(0, C)
-        turn(dh2, 2, 0, False)
-        turn(dh3, 3, 1, False)
-        first = [product(eng, 4 + 2 * eng, [(0, eng, 0)]) for eng in range(2)]
+        permute(0)
+        gw0 = gather_words(0, CH, 9 * T)
+        gw1 = gather_words(CH, C, 9 * T + 4 * CH)
+        permute(1)
+        gw2 = gather_words(C, S, 8 * T)
+        def whole(side, m):
+            return [(side, m, 0, C), (side, m, C, S)]
+
+        hidden(0, gw0[:])
+        hidden(1, gw1[:])
+        quantise(0, CH)
+        y0 = product(1, 4, [(0, 0, 0, CH), (0, 1, 0, CH)], 12 * T)
+        hidden(2, gw2[:, 0:CH])
+        quantise(CH, C)
+        y1 = product(1, 5, [(0, 0, CH, C), (0, 1, CH, C)])
+        hidden(3, gw2[:, CH:C])
         quantise(C, S)
-        scatter(0, 0, 0, 0, C, first[0][:])
-        second = [product(eng, 5 + 2 * eng, [(1, eng, 0)]) for eng in range(2)]
-        scatter(1, 0, 1, 0, C, first[1][:])
-        third = [product(eng, 4 + 2 * eng, [(0, eng, 1), (1, eng, 1)]) for eng in range(2)]
-        for eng in range(2):
-            scatter(eng, 1, eng, 0, C, second[eng][:])
-            scatter(eng, 0, eng, C, S, third[eng][:, 0:C])
-        fourth = [product(eng, 5 + 2 * eng, [(eng, 2, 0), (eng, 2, 1)]) for eng in range(2)]
-        for eng in range(2):
-            scatter(eng, 1, eng, C, S, third[eng][:, C:S])
+        for n, side in enumerate((1, 1)):
+            wins[side].append(late.tile([P, T], F32, name="late%d" % n, align_bytes=64, offset=4 * T * n))
+            nc.gpsimd.memset(wins[side][-1][:], 0.0)
+        scatter(1, 0, 0, 0, CH, y0[:, 0:CH])
+        scatter(1, 0, 1, 0, CH, y0[:, CH:C])
+        wins[0].append(late.tile([P, T], F32, name="late2", align_bytes=64, offset=12 * T))
+        nc.gpsimd.memset(wins[0][2][:], 0.0)
+        p0 = product(0, 6, whole(1, 0))
+        y2 = product(1, 0, [(0, 0, C, S), (0, 1, C, S)])
+        p1 = product(0, 7, whole(1, 1))
+        scatter(1, 0, 0, CH, C, y1[:, 0:CH])
+        scatter(1, 0, 1, CH, C, y1[:, CH:C])
+        scatter(0, 1, 0, 0, S, p0[:])
+        scatter(1, 0, 0, C, S, y2[:, 0:C])
         add_early(0)
+        p2 = product(1, 1, whole(1, 2))
+        x2 = product(1, 6, whole(0, 2))
+        scatter(1, 0, 1, C, S, y2[:, C:S])
+        scatter(0, 1, 1, 0, S, p1[:])
         add_early(1)
-        scatter(1, 1, 2, 0, C, fourth[1][:, 0:C])
-        fifth = [product(eng, 4 + 2 * eng, [(eng, 3, 0), (eng, 3, 1)]) for eng in range(2)]
-        scatter(0, 0, 2, 0, S, fourth[0][:])
-        scatter(1, 1, 2, C, S, fourth[1][:, C:S])
+        scatter(1, 1, 2, 0, C, p2[:, 0:C])
+        x3 = product(1, 7, whole(0, 3))
+        scatter(1, 1, 2, C, S, p2[:, C:S])
+        scatter(0, 0, 2, 0, S, x2[:])
         add_early(2)
-        scatter(0, 0, 3, 0, S, fifth[0][:])
-        scatter(1, 1, 3, 0, C, fifth[1][:, 0:C])
-        scatter(1, 1, 3, C, S, fifth[1][:, C:S])
+        p3 = product(1, 2, whole(1, 3))
+        scatter(0, 0, 3, 0, S, x3[:])
+        scatter(1, 1, 3, 0, C, p3[:, 0:C])
+        scatter(1, 1, 3, C, S, p3[:, C:S])
         m = K // P - 1
         for h in range(4):
             cols = slice(h * T // 4, (h + 1) * T // 4)

@@ -69,12 +69,10 @@ def tile_moe_dub_none_kernel(
             queue.dma_start(dys[32 * q : 32 * q + 4].bitcast(I32), dy_scales[0, 4 * q : 4 * q + 4, :].bitcast(I32))
 
         nc.gpsimd.memset(dys[:].bitcast(I32), 0)
-        nc.vector.memset(w2s[:].bitcast(I32), 0)
-        nc.vector.memset(zero[:], 0.0)
+        nc.gpsimd.memset(w2s[:].bitcast(I32), 0)
+        nc.gpsimd.memset(zero[:], 0.0)
+        nc.gpsimd.memset(wins[1][0][:], 0.0)
         zeros = zero[:, 0:1].to_broadcast([P, T])
-        nc.vector.tensor_copy(wins[0][0][:], zeros)
-        nc.vector.tensor_copy(wins[0][1][:], zeros)
-        nc.vector.tensor_copy(wins[1][0][:], zeros)
         nc.scalar.dma_start(w2w[0][:].bitcast(I32), w2t_words[0, 0].bitcast(I32))
         nc.sync.dma_start(tok[:], offs)
         load_dy_rows(nc.scalar, 0)
@@ -158,6 +156,8 @@ def tile_moe_dub_none_kernel(
 
         nc.vector.tensor_copy(gs[:], dys[:].indirect(tok[:]))
         permute(0)
+        nc.scalar.copy(wins[0][0][:], zeros)
+        nc.scalar.copy(wins[0][1][:], zeros)
         gw0 = gather_words(0, CH, 9 * T)
         gw1 = gather_words(CH, C, 9 * T + 4 * CH)
         permute(1)
@@ -181,21 +181,23 @@ def tile_moe_dub_none_kernel(
         scatter(1, 0, 1, 0, CH, y0[:, CH:C])
         wins[0].append(late.tile([P, T], F32, name="late2", align_bytes=64, offset=12 * T))
         nc.gpsimd.memset(wins[0][2][:], 0.0)
-        p0 = product(0, 6, whole(1, 0))
+        p0 = product(0, 6, [(1, 0, 0, C)])
+        q0 = product(0, 7, [(1, 0, C, S)])
         y2 = product(1, 0, [(0, 0, C, S), (0, 1, C, S)])
-        p1 = product(0, 7, whole(1, 1))
+        scatter(0, 1, 0, 0, C, p0[:])
+        p1 = product(0, 6, whole(1, 1))
         scatter(1, 0, 0, CH, C, y1[:, 0:CH])
         scatter(1, 0, 1, CH, C, y1[:, CH:C])
-        scatter(0, 1, 0, 0, S, p0[:])
+        scatter(0, 1, 0, C, S, q0[:])
         scatter(1, 0, 0, C, S, y2[:, 0:C])
         add_early(0)
         p2 = product(1, 1, whole(1, 2))
-        x2 = product(1, 6, whole(0, 2))
+        x2 = product(1, 7, whole(0, 2))
         scatter(1, 0, 1, C, S, y2[:, C:S])
         scatter(0, 1, 1, 0, S, p1[:])
         add_early(1)
         scatter(1, 1, 2, 0, C, p2[:, 0:C])
-        x3 = product(1, 7, whole(0, 3))
+        x3 = product(1, 6, whole(0, 3))
         scatter(1, 1, 2, C, S, p2[:, C:S])
         scatter(0, 0, 2, 0, S, x2[:])
         add_early(2)

@@ -50,7 +50,7 @@ def tile_moe_dub_none_kernel(
         quads = late.tile([P, 4 * S], BF16, name="quads", align_bytes=64, offset=2 * T)
         dqw = keep.tile([P, S], U32, name="dqw", align_bytes=64)
         dqs = keep.tile([P, S], U8, name="dqs", align_bytes=64)
-        wins = [[keep.tile([P, T], F32, name="win%d_%d" % (side, b)) for b in range(2 - side)] for side in range(2)]
+        wins = [[keep.tile([P, T], F32, name="win%d_%d" % (side, b)) for b in range(3 - 2 * side)] for side in range(2)]
         sums = [keep.tile([P, T], F32, name="sum%d" % m) for m in range(K // P)]
         banks = [ps.tile([P, BANK], F32, name="bank%d" % b) for b in range(8)]
 
@@ -71,7 +71,8 @@ def tile_moe_dub_none_kernel(
         nc.gpsimd.memset(dys[:].bitcast(I32), 0)
         nc.gpsimd.memset(w2s[:].bitcast(I32), 0)
         nc.gpsimd.memset(zero[:], 0.0)
-        nc.gpsimd.memset(wins[1][0][:], 0.0)
+        nc.gpsimd.memset(wins[0][2][:], 0.0)
+        nc.vector.memset(wins[1][0][:], 0.0)
         zeros = zero[:, 0:1].to_broadcast([P, T])
         nc.scalar.dma_start(w2w[0][:].bitcast(I32), w2t_words[0, 0].bitcast(I32))
         nc.sync.dma_start(tok[:], offs)
@@ -168,40 +169,38 @@ def tile_moe_dub_none_kernel(
         hidden(0, gw0[:])
         hidden(1, gw1[:])
         quantise(0, CH)
-        y0 = product(1, 4, [(0, 0, 0, CH), (0, 1, 0, CH)], 12 * T)
+        y0 = product(1, 4, [(0, 0, 0, CH), (0, 1, 0, CH)])
         hidden(2, gw2[:, 0:CH])
         quantise(CH, C)
         y1 = product(1, 5, [(0, 0, CH, C), (0, 1, CH, C)])
         hidden(3, gw2[:, CH:C])
+        x0 = product(0, 6, [(0, 2, 0, C)])
         quantise(C, S)
-        for n, side in enumerate((1, 1)):
-            wins[side].append(late.tile([P, T], F32, name="late%d" % n, align_bytes=64, offset=4 * T * n))
-            nc.gpsimd.memset(wins[side][-1][:], 0.0)
+        for n in range(2):
+            wins[1].append(late.tile([P, T], F32, name="late%d" % n, align_bytes=64, offset=4 * T * n))
+            nc.gpsimd.memset(wins[1][-1][:], 0.0)
         scatter(1, 0, 0, 0, CH, y0[:, 0:CH])
         scatter(1, 0, 1, 0, CH, y0[:, CH:C])
-        wins[0].append(late.tile([P, T], F32, name="late2", align_bytes=64, offset=12 * T))
-        nc.gpsimd.memset(wins[0][2][:], 0.0)
-        p0 = product(0, 6, [(1, 0, 0, C)])
-        q0 = product(0, 7, [(1, 0, C, S)])
+        scatter(0, 0, 2, 0, C, x0[:])
         y2 = product(1, 0, [(0, 0, C, S), (0, 1, C, S)])
-        scatter(0, 1, 0, 0, C, p0[:])
+        p0 = product(0, 7, whole(1, 0))
         p1 = product(0, 6, whole(1, 1))
         scatter(1, 0, 0, CH, C, y1[:, 0:CH])
         scatter(1, 0, 1, CH, C, y1[:, CH:C])
-        scatter(0, 1, 0, C, S, q0[:])
+        scatter(0, 1, 0, 0, S, p0[:])
         scatter(1, 0, 0, C, S, y2[:, 0:C])
         add_early(0)
         p2 = product(1, 1, whole(1, 2))
-        x2 = product(1, 7, whole(0, 2))
+        x2 = product(1, 7, [(0, 2, C, S)])
         scatter(1, 0, 1, C, S, y2[:, C:S])
         scatter(0, 1, 1, 0, S, p1[:])
         add_early(1)
         scatter(1, 1, 2, 0, C, p2[:, 0:C])
-        x3 = product(1, 6, whole(0, 3))
-        scatter(1, 1, 2, C, S, p2[:, C:S])
-        scatter(0, 0, 2, 0, S, x2[:])
-        add_early(2)
+        x3 = product(0, 6, whole(0, 3))
         p3 = product(1, 2, whole(1, 3))
+        scatter(1, 1, 2, C, S, p2[:, C:S])
+        scatter(0, 0, 2, C, S, x2[:])
+        add_early(2)
         scatter(0, 0, 3, 0, S, x3[:])
         scatter(1, 1, 3, 0, C, p3[:, 0:C])
         scatter(1, 1, 3, C, S, p3[:, C:S])

@@ -36,10 +36,10 @@ def tile_moe_dub_none_kernel(
         par = keep.tile([P, S // 16], U16, name="par")
         dyw = keep.tile([P, T], I32, name="dyw", align_bytes=64)
         dys = keep.tile([P, T], U8, name="dys", align_bytes=64)
-        w2w = [keep.tile([P, 2 * H], U8, name="w2w%d" % e, align_bytes=64) for e in range(E)]
+        w2w = [late.tile([P, 2 * H], U8, name="w2w%d" % e, align_bytes=64, offset=(16 + 2 * e) * T) for e in range(E)]
         w2p = [keep.tile([P, 2 * H], U8, name="w2p%d" % e, align_bytes=64) for e in range(E)]
         w2q = [keep.tile([P, H], U8, name="w2q%d" % e, align_bytes=64) for e in range(E)]
-        w1w = keep.tile([P, E, 2 * K], U8, name="w1w", align_bytes=64)
+        w1w = late.tile([P, E, 2 * K], U8, name="w1w", align_bytes=64, offset=16 * T)
         wpw = keep.tile([P, E, 2 * K], U8, name="wpw", align_bytes=64)
         w2s = late.tile([P, E, H], U8, name="w2s", align_bytes=64, offset=8 * T)
         w1s = keep.tile([P, E, K], U8, name="w1s", align_bytes=64)
@@ -85,7 +85,8 @@ def tile_moe_dub_none_kernel(
             load_rows(nc.sync, w2s, w2t_scales, q)
         nc.sync.dma_start(w2w[1][:].bitcast(I32), w2t_words[1, 0].bitcast(I32))
         nc.sync.dma_start(gates[:], gate)
-        load_matrix(w1w, w1s, w1t_words, w1t_scales)
+        for q in range(4):
+            load_rows(nc.sync, w1s, w1t_scales, q)
         nc.sync.dma_start(par[:], offs2)
         load_matrix(wpw, wps, wpt_words, wpt_scales)
 
@@ -151,12 +152,15 @@ def tile_moe_dub_none_kernel(
             else:
                 nc.scalar.activation(target, ys, COPY)
 
-        def add_early(m):
-            nc.gpsimd.tensor_tensor(sums[m][:], wins[0][m % 3][:], wins[1][m % 3][:], ADD)
-            nc.sync.dma_start(out[m * P : (m + 1) * P, :], sums[m][:])
+        def add_early(m, pieces):
+            for h in range(pieces):
+                cols = slice(h * T // pieces, (h + 1) * T // pieces)
+                nc.gpsimd.tensor_tensor(sums[m][:, cols], wins[0][m % 3][:, cols], wins[1][m % 3][:, cols], ADD)
+                nc.sync.dma_start(out[m * P : (m + 1) * P, cols], sums[m][:, cols])
 
         nc.vector.tensor_copy(gs[:], dys[:].indirect(tok[:]))
         permute(0)
+        nc.scalar.dma_start(w1w[:].bitcast(I32), w1t_words[:, 0].rearrange("e p n -> p e n").bitcast(I32))
         nc.scalar.copy(wins[0][0][:], zeros)
         nc.scalar.copy(wins[0][1][:], zeros)
         gw0 = gather_words(0, CH, 9 * T)
@@ -169,38 +173,38 @@ def tile_moe_dub_none_kernel(
         hidden(0, gw0[:])
         hidden(1, gw1[:])
         quantise(0, CH)
-        y0 = product(1, 4, [(0, 0, 0, CH), (0, 1, 0, CH)])
+        y0 = product(1, 4, [(0, 1, 0, CH), (0, 2, 0, CH)])
         hidden(2, gw2[:, 0:CH])
         quantise(CH, C)
-        y1 = product(1, 5, [(0, 0, CH, C), (0, 1, CH, C)])
+        y1 = product(1, 5, [(0, 1, CH, C), (0, 2, CH, C)])
         hidden(3, gw2[:, CH:C])
-        x0 = product(0, 6, [(0, 2, 0, C)])
+        x0 = product(0, 6, [(0, 0, 0, C)])
         quantise(C, S)
         for n in range(2):
             wins[1].append(late.tile([P, T], F32, name="late%d" % n, align_bytes=64, offset=4 * T * n))
             nc.gpsimd.memset(wins[1][-1][:], 0.0)
-        scatter(1, 0, 0, 0, CH, y0[:, 0:CH])
-        scatter(1, 0, 1, 0, CH, y0[:, CH:C])
-        scatter(0, 0, 2, 0, C, x0[:])
-        y2 = product(1, 0, [(0, 0, C, S), (0, 1, C, S)])
-        p0 = product(0, 7, whole(1, 0))
+        scatter(1, 0, 1, 0, CH, y0[:, 0:CH])
+        scatter(1, 0, 2, 0, CH, y0[:, CH:C])
+        scatter(0, 0, 0, 0, C, x0[:])
+        x1 = product(0, 7, [(0, 0, C, S)])
+        p0 = product(1, 0, whole(1, 0))
+        scatter(1, 0, 1, CH, C, y1[:, 0:CH])
+        scatter(1, 0, 2, CH, C, y1[:, CH:C])
+        scatter(0, 0, 0, C, S, x1[:])
         p1 = product(0, 6, whole(1, 1))
-        scatter(1, 0, 0, CH, C, y1[:, 0:CH])
-        scatter(1, 0, 1, CH, C, y1[:, CH:C])
-        scatter(0, 1, 0, 0, S, p0[:])
-        scatter(1, 0, 0, C, S, y2[:, 0:C])
-        add_early(0)
-        p2 = product(1, 1, whole(1, 2))
-        x2 = product(1, 7, [(0, 2, C, S)])
-        scatter(1, 0, 1, C, S, y2[:, C:S])
+        p2 = product(0, 7, whole(1, 2))
+        scatter(1, 1, 0, 0, C, p0[:, 0:C])
+        y2 = product(1, 0, [(0, 1, C, S), (0, 2, C, S)])
+        scatter(1, 1, 0, C, S, p0[:, C:S])
+        add_early(0, 1)
         scatter(0, 1, 1, 0, S, p1[:])
-        add_early(1)
-        scatter(1, 1, 2, 0, C, p2[:, 0:C])
-        x3 = product(0, 6, whole(0, 3))
-        p3 = product(1, 2, whole(1, 3))
-        scatter(1, 1, 2, C, S, p2[:, C:S])
-        scatter(0, 0, 2, C, S, x2[:])
-        add_early(2)
+        scatter(1, 0, 1, C, S, y2[:, 0:C])
+        add_early(1, 1)
+        x3 = product(1, 6, whole(0, 3))
+        p3 = product(1, 1, whole(1, 3))
+        scatter(1, 0, 2, C, S, y2[:, C:S])
+        scatter(0, 1, 2, 0, S, p2[:])
+        add_early(2, 2)
         scatter(0, 0, 3, 0, S, x3[:])
         scatter(1, 1, 3, 0, C, p3[:, 0:C])
         scatter(1, 1, 3, C, S, p3[:, C:S])

@@ -187,11 +187,12 @@ def tile_moe_dub_none_kernel(
         scatter(1, 0, 2, 0, CH, y0[:, CH:C])
         scatter(0, 0, 0, 0, C, x0[:])
         x1 = product(0, 7, [(0, 0, C, S)])
+        x3 = product(0, 2, whole(0, 3))
         p0 = product(1, 0, whole(1, 0))
+        p1 = product(1, 6, whole(1, 1))
         scatter(1, 0, 1, CH, C, y1[:, 0:CH])
         scatter(1, 0, 2, CH, C, y1[:, CH:C])
         scatter(0, 0, 0, C, S, x1[:])
-        p1 = product(0, 6, whole(1, 1))
         p2 = product(0, 7, whole(1, 2))
         scatter(1, 1, 0, 0, C, p0[:, 0:C])
         y2 = product(1, 0, [(0, 1, C, S), (0, 2, C, S)])
@@ -200,7 +201,6 @@ def tile_moe_dub_none_kernel(
         scatter(0, 1, 1, 0, S, p1[:])
         scatter(1, 0, 1, C, S, y2[:, 0:C])
         add_early(1, 1)
-        x3 = product(1, 6, whole(0, 3))
         p3 = product(1, 1, whole(1, 3))
         scatter(1, 0, 2, C, S, y2[:, C:S])
         scatter(0, 1, 2, 0, S, p2[:])

from contextlib import ExitStack

import concourse.mybir as mybir

K, T, E, C, H, N = 512, 1024, 2, 256, 512, 512
S = E * C
FLOPS = 2 * S * (N * H + 2 * H * K)

F32 = mybir.dt.float32
BF16 = mybir.dt.bfloat16
I32 = mybir.dt.int32
U32 = mybir.dt.uint32
U16 = mybir.dt.uint16
U8 = mybir.dt.uint8
FP8X4 = mybir.dt.float8_e4m3fn_x4
FP4X4 = mybir.dt.float4_e2m1fn_x4
COPY = mybir.ActivationFunctionType.Copy
ADD = mybir.AluOpType.add
MULT = mybir.AluOpType.mult

P = 128
CH = 128
BANK = 512


def tile_moe_dub_none_kernel(
    tc, dy_words, dy_scales, w2t_words, w2t_scales, w1t_words, w1t_scales, wpt_words, wpt_scales, gate, offs, offs2, out
):
    nc = tc.nc
    with ExitStack() as ctx:
        keep = ctx.enter_context(tc.tile_pool(name="keep", bufs=1))
        late = ctx.enter_context(tc.tile_pool(name="late", bufs=1))
        ps = ctx.enter_context(tc.psum_pool(name="ps", bufs=1))

        tok = keep.tile([P, S // 16], U16, name="tok")
        par = keep.tile([P, S // 16], U16, name="par")
        dyw = keep.tile([P, T], I32, name="dyw", align_bytes=64)
        dys = keep.tile([P, T], U8, name="dys", align_bytes=64)
        w2w = [late.tile([P, 2 * H], U8, name="w2w%d" % e, align_bytes=64, offset=(16 + 2 * e) * T) for e in range(E)]
        w2p = [keep.tile([P, 2 * H], U8, name="w2p%d" % e, align_bytes=64) for e in range(E)]
        w2q = [keep.tile([P, H], U8, name="w2q%d" % e, align_bytes=64) for e in range(E)]
        w1w = late.tile([P, E, 2 * K], U8, name="w1w", align_bytes=64, offset=16 * T)
        wpw = keep.tile([P, E, 2 * K], U8, name="wpw", align_bytes=64)
        w2s = late.tile([P, E, H], U8, name="w2s", align_bytes=64, offset=8 * T)
        w1s = keep.tile([P, E, K], U8, name="w1s", align_bytes=64)
        wps = keep.tile([P, E, K], U8, name="wps", align_bytes=64)
        gates = keep.tile([P, S], F32, name="gates")
        zero = keep.tile([P, 8], F32, name="zero")
        gs = keep.tile([P, S], U8, name="gs", align_bytes=64)
        quads = late.tile([P, 4 * S], BF16, name="quads", align_bytes=64, offset=2 * T)
        dqw = keep.tile([P, S], U32, name="dqw", align_bytes=64)
        dqs = keep.tile([P, S], U8, name="dqs", align_bytes=64)
        wins = [[keep.tile([P, T], F32, name="win%d_%d" % (side, b)) for b in range(3 - 2 * side)] for side in range(2)]
        sums = [keep.tile([P, T], F32, name="sum%d" % m) for m in range(K // P)]
        banks = [ps.tile([P, BANK], F32, name="bank%d" % b) for b in range(8)]

        def load_rows(queue, tile, scales, q):
            queue.dma_start(
                tile[32 * q : 32 * q + 4].bitcast(I32),
                scales[:, 0, 4 * q : 4 * q + 4, :].rearrange("e r n -> r e n").bitcast(I32),
            )

        def load_matrix(wtile, stile, words, scales):
            nc.sync.dma_start(wtile[:].bitcast(I32), words[:, 0].rearrange("e p n -> p e n").bitcast(I32))
            for q in range(4):
                load_rows(nc.sync, stile, scales, q)

        def load_dy_rows(queue, q):
            queue.dma_start(dys[32 * q : 32 * q + 4].bitcast(I32), dy_scales[0, 4 * q : 4 * q + 4, :].bitcast(I32))

        nc.gpsimd.memset(dys[:].bitcast(I32), 0)
        nc.gpsimd.memset(w2s[:].bitcast(I32), 0)
        nc.gpsimd.memset(zero[:], 0.0)
        nc.gpsimd.memset(wins[0][2][:], 0.0)
        nc.vector.memset(wins[1][0][:], 0.0)
        zeros = zero[:, 0:1].to_broadcast([P, T])
        nc.scalar.dma_start(w2w[0][:].bitcast(I32), w2t_words[0, 0].bitcast(I32))
        nc.sync.dma_start(tok[:], offs)
        load_dy_rows(nc.scalar, 0)
        load_dy_rows(nc.sync, 2)
        load_dy_rows(nc.scalar, 1)
        load_dy_rows(nc.sync, 3)
        nc.scalar.dma_start(dyw[:], dy_words[0].rearrange("p t d -> p (t d)").bitcast(I32))
        for q in range(4):
            load_rows(nc.sync, w2s, w2t_scales, q)
        nc.sync.dma_start(w2w[1][:].bitcast(I32), w2t_words[1, 0].bitcast(I32))
        nc.sync.dma_start(gates[:], gate)
        for q in range(4):
            load_rows(nc.sync, w1s, w1t_scales, q)
        nc.sync.dma_start(par[:], offs2)
        load_matrix(wpw, wps, wpt_words, wpt_scales)

        def permute(e):
            nc.scalar.copy(
                w2p[e][:].bitcast(U16).rearrange("p (t m) -> p t m", t=4),
                w2w[e][:].bitcast(U16).rearrange("p (m t) -> p t m", t=4),
            )
            nc.vector.tensor_copy(
                w2q[e][:].rearrange("p (t m) -> p t m", t=4), w2s[:, e, :].rearrange("p (m t) -> p t m", t=4)
            )

        def gather_words(a, b, offset):
            gw = late.tile([P, b - a], U32, name="gw%d" % a, align_bytes=64, offset=offset)
            nc.vector.tensor_copy(gw[:], dyw[:].bitcast(U32).indirect(tok[:, a // 16 : b // 16]))
            return gw

        def hidden(c, gw):
            e = c * CH // C
            acc = banks[c][:].rearrange("p (t s) -> p t s", t=4)
            for t in range(4):
                nc.tensor.matmul_mx(
                    out=acc[:, t, :], lhsT=w2p[e][:, 2 * P * t : 2 * P * (t + 1)].bitcast(FP4X4),
                    lhsT_scale=w2q[e][:, P * t : P * (t + 1)],
                    rhs=gw.bitcast(FP8X4), rhs_scale=gs[:, c * CH : (c + 1) * CH], start=True, stop=True,
                )
            g = gates[:, c * CH : (c + 1) * CH].unsqueeze(2).to_broadcast([P, CH, 4])
            dst = quads[:, 4 * CH * c : 4 * CH * (c + 1)].rearrange("p (s t) -> p s t", t=4)
            nc.vector.tensor_tensor(dst, acc.rearrange("p t s -> p s t"), g, MULT)

        def quantise(a, b):
            nc.vector.quantize_mx(out=dqw[:, a:b].bitcast(FP8X4), scales=dqs[:, a:b], in_=quads[:, 4 * a : 4 * b])

        sides = ((w1w, w1s, tok), (wpw, wps, par))

        def product(eng, at, jobs, offset=None):
            y = banks[at]
            col = 0
            for side, m, a, b in jobs:
                ww, ws = sides[side][:2]
                e = a // C
                nc.tensor.matmul_mx(
                    out=y[:, col : col + b - a], lhsT=ww[:, e, 2 * P * m : 2 * P * (m + 1)].bitcast(FP4X4),
                    lhsT_scale=ws[:, e, P * m : P * (m + 1)],
                    rhs=dqw[:, a:b].bitcast(FP8X4), rhs_scale=dqs[:, a:b], start=True, stop=True,
                )
                col += b - a
            name = "ys%d_%d_%d" % jobs[0][:3]
            if offset is None:
                ys = keep.tile([P, col], F32, name=name)
            else:
                ys = late.tile([P, col], F32, name=name, align_bytes=64, offset=offset)
            if eng == 0:
                nc.vector.tensor_copy(ys[:], y[:, 0:col])
            else:
                nc.scalar.copy(ys[:], y[:, 0:col])
            return ys

        def scatter(eng, side, m, a, b, ys):
            target = wins[side][m % 3][:].indirect(sides[side][2][:, a // 16 : b // 16])
            if eng == 0:
                nc.vector.tensor_copy(target, ys)
            else:
                nc.scalar.activation(target, ys, COPY)

        def add_early(m, pieces):
            for h in range(pieces):
                cols = slice(h * T // pieces, (h + 1) * T // pieces)
                nc.gpsimd.tensor_tensor(sums[m][:, cols], wins[0][m % 3][:, cols], wins[1][m % 3][:, cols], ADD)
                nc.sync.dma_start(out[m * P : (m + 1) * P, cols], sums[m][:, cols])

        nc.vector.tensor_copy(gs[:], dys[:].indirect(tok[:]))
        permute(0)
        nc.scalar.dma_start(w1w[:].bitcast(I32), w1t_words[:, 0].rearrange("e p n -> p e n").bitcast(I32))
        nc.scalar.copy(wins[0][0][:], zeros)
        nc.scalar.copy(wins[0][1][:], zeros)
        gw0 = gather_words(0, CH, 9 * T)
        gw1 = gather_words(CH, C, 9 * T + 4 * CH)
        permute(1)
        gw2 = gather_words(C, S, 8 * T)
        def whole(side, m):
            return [(side, m, 0, C), (side, m, C, S)]

        hidden(0, gw0[:])
        hidden(1, gw1[:])
        quantise(0, CH)
        y0 = product(1, 4, [(0, 1, 0, CH), (0, 2, 0, CH)])
        hidden(2, gw2[:, 0:CH])
        quantise(CH, C)
        y1 = product(1, 5, [(0, 1, CH, C), (0, 2, CH, C)])
        hidden(3, gw2[:, CH:C])
        x0 = product(0, 6, [(0, 0, 0, C)])
        quantise(C, S)
        for n in range(2):
            wins[1].append(late.tile([P, T], F32, name="late%d" % n, align_bytes=64, offset=4 * T * n))
            nc.gpsimd.memset(wins[1][-1][:], 0.0)
        scatter(1, 0, 1, 0, CH, y0[:, 0:CH])
        scatter(1, 0, 2, 0, CH, y0[:, CH:C])
        scatter(0, 0, 0, 0, C, x0[:])
        x1 = product(0, 7, [(0, 0, C, S)])
        x3 = product(0, 2, whole(0, 3))
        p0 = product(1, 0, whole(1, 0))
        p1 = product(1, 6, whole(1, 1))
        scatter(1, 0, 1, CH, C, y1[:, 0:CH])
        scatter(1, 0, 2, CH, C, y1[:, CH:C])
        scatter(0, 0, 0, C, S, x1[:])
        p2 = product(0, 7, whole(1, 2))
        scatter(1, 1, 0, 0, C, p0[:, 0:C])
        y2 = product(1, 0, [(0, 1, C, S), (0, 2, C, S)])
        scatter(1, 1, 0, C, S, p0[:, C:S])
        add_early(0, 1)
        scatter(0, 1, 1, 0, S, p1[:])
        scatter(1, 0, 1, C, S, y2[:, 0:C])
        add_early(1, 1)
        p3 = product(1, 1, whole(1, 3))
        scatter(1, 0, 2, C, S, y2[:, C:S])
        scatter(0, 1, 2, 0, S, p2[:])
        add_early(2, 2)
        scatter(0, 0, 3, 0, S, x3[:])
        scatter(1, 1, 3, 0, C, p3[:, 0:C])
        scatter(1, 1, 3, C, S, p3[:, C:S])
        m = K // P - 1
        for h in range(4):
            cols = slice(h * T // 4, (h + 1) * T // 4)
            nc.vector.tensor_tensor(sums[m][:, cols], wins[0][m % 3][:, cols], wins[1][m % 3][:, cols], ADD)
            nc.sync.dma_start(out[m * P : (m + 1) * P, cols], sums[m][:, cols])
